import numpy as np
import ml_dtypes


def mxq(x, axis, fmt="e4m3"):
    dtype, down = {"e4m3": (ml_dtypes.float8_e4m3fn, 7), "e5m2": (ml_dtypes.float8_e5m2, 14)}[fmt]
    v = np.moveaxis(np.asarray(x, np.float32).astype(ml_dtypes.bfloat16).astype(np.float64), axis, -1)
    blocks = v.reshape(v.shape[:-1] + (-1, 32))
    amax = np.abs(blocks).max(-1, keepdims=True)
    byte = np.maximum(np.where(amax > 0, np.frexp(amax)[1] - 1 + 127, 0) - down, 1)
    scale = np.exp2(byte - 127.0)
    codes = (blocks / scale).astype(np.float32).astype(dtype).astype(np.float64)
    return np.moveaxis((codes * scale).reshape(v.shape), -1, axis)


WIDE = False


def mx_kscale(k):
    if not WIDE:
        return np.ones(k)
    levels = np.array([10, -10, 5, -5, 0])
    if k % 512:
        return np.exp2(np.random.permutation(np.resize(levels, k // 32))).repeat(32)
    a = np.empty((k // 512, 16))
    for p in range(k // 512):
        a[p, :8] = np.random.permutation(np.resize(levels, 8))
        for g in range(8):
            far = levels[np.abs(levels - a[p, g]) >= 10]
            a[p, g + 8] = far[np.random.randint(len(far))]
    return np.exp2(a.ravel()).repeat(32)


BF16 = ml_dtypes.bfloat16


def bf(x):
    return np.asarray(x, np.float32).astype(BF16)


def f64(x):
    return np.asarray(x).astype(np.float64)


E2M1 = np.array([0.0, 0.5, 1.0, 1.5, 2.0, 3.0, 4.0, 6.0, -0.0, -0.5, -1.0, -1.5, -2.0, -3.0, -4.0, -6.0])


def pack_weight(w, fmt):
    k, n = w.shape
    w = f64(bf(w)).reshape(k // 32, 32, n)
    amax = np.abs(w).max(1)
    if fmt == "e4m3":
        byte = np.frexp(amax)[1] - 1 + 127 - 7
    else:
        mant, ex = np.frexp(amax / 6.0)
        byte = np.where(mant > 0.5, ex, ex - 1) + 127
    byte = np.clip(np.where(amax > 0, byte, 1), 1, 254)
    scaled = (w * np.exp2(127.0 - byte)[:, None, :]).reshape(k, n).astype(np.float32)
    by_word = np.ascontiguousarray(scaled.reshape(k // 512, 128, 4, n).transpose(0, 1, 3, 2))
    if fmt == "e4m3":
        words = by_word.astype(ml_dtypes.float8_e4m3fn).view(np.uint8)
    else:
        c = by_word.astype(ml_dtypes.float4_e2m1fn).view(np.uint8) & 0xF
        words = c[..., 0::2] | (c[..., 1::2] << 4)
    return np.ascontiguousarray(words), np.ascontiguousarray(byte.astype(np.uint8).reshape(k // 512, 16, n))


def unpack_weight(words, scales, fmt):
    g, p, n, _ = words.shape
    if fmt == "e4m3":
        vals = np.ascontiguousarray(words).view(ml_dtypes.float8_e4m3fn).astype(np.float64)
    else:
        nib = np.empty((g, p, n, 4), np.uint8)
        nib[..., 0::2] = words & 0xF
        nib[..., 1::2] = words >> 4
        vals = E2M1[nib]
    vals = vals * np.repeat(np.exp2(scales.astype(np.float64) - 127.0), 8, axis=1)[..., None]
    return vals.transpose(0, 1, 3, 2).reshape(g * 512, n)


B, T, D, P, F, NA, NC, STRIDE = 2, 512, 1024, 512, 2048, 4, 3, 2


def look_back(p, s):
    n = p.shape[1]
    padded = np.pad(p, ((0, 0), (s, 0), (0, 0)))
    return padded[:, :n, :]


def look_ahead(p, s):
    n = p.shape[1]
    padded = np.pad(p, ((0, 0), (0, s), (0, 0)))
    return padded[:, s:s + n, :]


def draw0():
    s, t = mx_kscale(D), mx_kscale(P)
    x = bf(np.random.standard_normal((B, T, D)) * s)
    skip = bf(np.random.standard_normal((B, T, P)) * t)
    v_words, v_scales = pack_weight(np.random.standard_normal((D, P)) / np.sqrt(D) / s[:, None] * t, "e4m3")
    a = bf(0.3 * np.random.standard_normal((NA, P)))
    c = bf(0.3 * np.random.standard_normal((NC, P)))
    u_words, u_scales = pack_weight(np.random.standard_normal((P, F)) / np.sqrt(P) / t[:, None], "e4m3")
    b = bf(0.3 * np.random.standard_normal(F))
    return {
        "x": x,
        "skip": skip,
        "v_words": v_words,
        "v_scales": v_scales,
        "a": a,
        "c": c,
        "u_words": u_words,
        "u_scales": u_scales,
        "b": b,
    }


def core(x, skip, v_words, v_scales, a, c, u_words, u_scales, b):
    a, c = f64(a), f64(c)
    p = mxq(f64(x), 2, "e4m3") @ unpack_weight(v_words, v_scales, "e4m3")

    back = np.zeros_like(p)
    for i in range(a.shape[0]):
        back = back + a[i] * look_back(p, STRIDE * i)

    ahead = np.zeros_like(p)
    for j in range(c.shape[0]):
        ahead = ahead + c[j] * look_ahead(p, STRIDE * (j + 1))

    m = f64(skip) + p + back + ahead

    return np.maximum((mxq(m, 2, "e4m3") @ unpack_weight(u_words, u_scales, "e4m3")) + f64(b), 0.0)


def e4m3fn_bytes(y):
    return np.clip(np.asarray(y, np.float64), -448.0, 448.0).astype(np.float32).astype(ml_dtypes.float8_e4m3fn).view(np.uint8)


def e4m3fn_values(b):
    return np.asarray(b, np.uint8).view(ml_dtypes.float8_e4m3fn).astype(np.float64)


def setup_inputs():
    d = draw0()
    x0 = np.asarray(d['x']).astype(np.float64)
    s = (np.max(np.abs(x0), axis=(0, 1), keepdims=True) / 448.0).astype(np.float32)
    out = {}
    for k, v in d.items():
        if k == 'x':
            out['x_bytes'] = e4m3fn_bytes(x0 / s.astype(np.float64))
            out['x_scale'] = s
        else:
            out[k] = v
    return out


def reference(x_bytes, x_scale, skip, v_words, v_scales, a, c, u_words, u_scales, b):
    return core(e4m3fn_values(x_bytes) * x_scale.astype(np.float64), skip, v_words, v_scales, a, c, u_words, u_scales, b)

@@ -1,0 +1,370 @@
+from contextlib import ExitStack
+
+import concourse.mybir as mybir
+from concourse.masks import make_identity
+
+F32 = mybir.dt.float32
+BF16 = mybir.dt.bfloat16
+I32 = mybir.dt.int32
+U32 = mybir.dt.uint32
+U8 = mybir.dt.uint8
+FP8 = mybir.dt.float8_e4m3fn
+FP8X4 = mybir.dt.float8_e4m3fn_x4
+ALU = mybir.AluOpType
+ACT = mybir.ActivationFunctionType
+
+P = 128
+SEQS, FRAMES, D, C, F = 2, 512, 1024, 512, 2048
+HALF = 256
+BLOCKS = C // P
+PASSES = D // 512
+STRIDE = 2
+FLOPS = 2 * SEQS * FRAMES * (D * C + C * F)
+BIG = 3.0e38
+
+PLANES = (((0, 0), (1, 2)), ((4, -2), (2, 4)), ((5, -4), (3, 6)), ((6, -6),))
+STEPS = 16
+HELP = {0: (3, "scalar"), 1: (4, "vector"), 2: (5, "scalar"), 3: (6, "vector"), 4: (7, "scalar")}
+
+
+def tile_deepfsmnstridedmemoryblock_w8_kernel(
+    tc, x_bytes, x_scale, skip, v_words, v_scales, a, c, u_words, u_scales, b, out
+):
+    nc = tc.nc
+    with ExitStack() as ctx:
+        keep = ctx.enter_context(tc.tile_pool(name="keep", bufs=1))
+        work = ctx.enter_context(tc.tile_pool(name="work", bufs=3))
+        psum = ctx.enter_context(tc.psum_pool(name="psum", bufs=1))
+
+        xb8 = {}
+
+        def load_x(n, first, count):
+            t = keep.tile([P, count, D], U8, name=f"xbytes{n}{first}")
+            nc.sync.dma_start(
+                out=t[:],
+                in_=x_bytes[n, P * first : P * (first + count), :].rearrange("(r p) k -> p r k", p=P),
+            )
+            for r in range(count):
+                xb8[4 * n + first + r] = t[:, r, :]
+
+        load_x(0, 0, 1)
+        xs = keep.tile([P, PASSES, 4], F32, name="xs")
+        with nc.allow_non_contiguous_dma(reason="16-byte runs of the input scales"):
+            nc.sync.dma_start(
+                out=xs[:], in_=x_scale.rearrange("o q (g p t) -> p (o q g) t", p=P, t=4)
+            )
+        rows = keep.tile([P, P], BF16, name="rows")
+        nc.vector.memset(rows[:], 0.0)
+        nc.sync.dma_start(out=rows[0:16, :], in_=a.rearrange("s (j q) -> (s j) q", q=P))
+        nc.sync.dma_start(out=rows[16:28, :], in_=c.rearrange("s (j q) -> (s j) q", q=P))
+        load_x(0, 1, 1)
+        load_x(0, 2, 2)
+        vq = keep.tile([P, PASSES, C], U32, name="vq", align_bytes=64)
+        nc.sync.dma_start(
+            out=vq[:].bitcast(I32),
+            in_=v_words.rearrange("g p n t -> p g (n t)").bitcast(I32),
+        )
+        vs = keep.tile([P, C], U8, name="vs", align_bytes=64)
+        nc.vector.memset(vs[:].bitcast(I32), 0)
+        for q in range(4):
+            nc.sync.dma_start(
+                out=vs[32 * q : 32 * q + 8, :].bitcast(I32),
+                in_=v_scales[:, 4 * q : 4 * q + 4, :].bitcast(I32),
+            )
+        load_x(1, 0, 2)
+        load_x(1, 2, 2)
+        sk = {}
+        for n in range(SEQS):
+            sk[n] = keep.tile([P, 4, C], BF16, name=f"skip{n}")
+            nc.sync.dma_start(out=sk[n][:], in_=skip[n].rearrange("(i p) c -> p i c", p=P))
+            if n == 0:
+                uq = keep.tile([P, F], U32, name="uq", align_bytes=64)
+                nc.sync.dma_start(
+                    out=uq[:].bitcast(I32), in_=u_words[0].rearrange("p n t -> p (n t)").bitcast(I32)
+                )
+                us = keep.tile([P, F], U8, name="us", align_bytes=64)
+                nc.vector.memset(us[:].bitcast(I32), 0)
+                for q in range(4):
+                    nc.sync.dma_start(
+                        out=us[32 * q : 32 * q + 4, :].bitcast(I32),
+                        in_=u_scales[0, 4 * q : 4 * q + 4, :].bitcast(I32),
+                    )
+                bias = keep.tile([P, F], BF16, name="bias")
+                nc.sync.dma_start(out=bias[:], in_=b.partition_broadcast(P))
+
+        ident = keep.tile([P, P], F32, name="ident")
+        make_identity(nc, ident[:])
+        ident16 = keep.tile([P, P], BF16, name="ident16")
+
+        y = {}
+        for n in range(SEQS):
+            for j in range(BLOCKS):
+                t = keep.tile([P, len(PLANES), FRAMES], F32, name=f"y{n}{j}")
+                for k, taps in enumerate(PLANES):
+                    d = taps[0][1]
+                    if d < 0:
+                        nc.gpsimd.memset(t[:, k, FRAMES + d : FRAMES], 0.0)
+                y[n, j] = t
+
+        w = keep.tile([P, 28], F32, name="w")
+        rows32 = keep.tile([P, P], F32, name="rows32")
+
+        def weights():
+            nc.vector.tensor_copy(out=rows32[:], in_=rows[:])
+            wt = psum.tile([P, 512], F32, name="turn", bufs=1)
+            nc.tensor.transpose(wt[:, 0:P], rows32[:], ident[:])
+            nc.vector.tensor_copy(out=w[:, 4:28], in_=wt[:, 4:28])
+            nc.vector.tensor_scalar(out=w[:, 0:4], in0=wt[:, 0:4], scalar1=1.0, scalar2=None, op0=ALU.add)
+            nc.vector.tensor_copy(out=ident16[:], in_=ident[:])
+
+        xq, xqs = {}, {}
+        for n in range(SEQS):
+            xq[n] = keep.tile([P, PASSES, FRAMES], U32, name=f"xq{n}", align_bytes=64)
+            xqs[n] = keep.tile([P, PASSES, FRAMES], U8, name=f"xqs{n}", align_bytes=64)
+
+        x16, xbank, xg = {}, {}, {}
+
+        def cast(r, engine):
+            x16[r] = work.tile([P, D], BF16, name="x16", bufs=3)
+            src = xb8[r].bitcast(FP8)
+            if engine == "vector":
+                nc.vector.tensor_copy(out=x16[r][:], in_=src)
+            else:
+                nc.scalar.copy(out=x16[r][:], in_=src)
+
+        def turn_x(r, tag):
+            words = x16[r][:].bitcast(F32)
+            xbank[r] = psum.tile([P, 512], F32, name=tag, bufs=1 if tag == "turn" else 2)
+            for g in range(PASSES):
+                for u in range(2):
+                    nc.tensor.transpose(
+                        xbank[r][:, 256 * g + 128 * u : 256 * g + 128 * u + 128],
+                        words[:, 256 * g + u : 256 * g + 256 : 2],
+                        ident[:],
+                    )
+
+        def scale_x(r):
+            xg[r] = work.tile([P, PASSES, P, 4], BF16, name="xg", bufs=2, align_bytes=64)
+            for g in range(PASSES):
+                nc.vector.tensor_tensor(
+                    out=xg[r][:, g, :, :].rearrange("p r (u e) -> p r u e", u=2),
+                    in0=xbank[r][:, 256 * g : 256 * g + 256]
+                    .bitcast(BF16)
+                    .rearrange("p (u r e) -> p r u e", u=2, e=2),
+                    in1=xs[:, g, :]
+                    .rearrange("p (o u e) -> p o u e", o=1, u=2)
+                    .to_broadcast([P, P, 2, 2]),
+                    op=ALU.mult,
+                )
+
+        def quantize_x(r):
+            n, i = divmod(r, 4)
+            for g in range(PASSES):
+                nc.vector.quantize_mx(
+                    out=xq[n][:, g, P * i : P * i + P].bitcast(FP8X4),
+                    scales=xqs[n][:, g, P * i : P * i + P],
+                    in_=xg[r][:, g, :, :].rearrange("p r k -> p (r k)"),
+                )
+
+        proj = {}
+
+        def project(s):
+            half, j = divmod(s, BLOCKS)
+            n, h = divmod(half, 2)
+            proj[s] = psum.tile([P, FRAMES], F32, name="proj", bufs=3)
+            for lo, hi in (((0, 256), (256, 384)), ((128, 256), (256, 512)))[h]:
+                for g in range(PASSES):
+                    nc.tensor.matmul_mx(
+                        out=proj[s][:, lo:hi],
+                        lhsT=vq[:, g, P * j : P * j + P].bitcast(FP8X4),
+                        lhsT_scale=vs[4 * g : P, P * j : P * j + P],
+                        rhs=xq[n][:, g, lo:hi].bitcast(FP8X4),
+                        rhs_scale=xqs[n][:, g, lo:hi],
+                        start=(g == 0),
+                        stop=(g == PASSES - 1),
+                    )
+
+        def tap(s, plane, which):
+            half, j = divmod(s, BLOCKS)
+            n, h = divmod(half, 2)
+            row, d = PLANES[plane][which]
+            lo, hi = max(HALF * h, d), min(HALF * h + HALF, FRAMES + d)
+            dst = y[n, j][:, plane, lo:hi]
+            src = proj[s][:, lo - d : hi - d]
+            wc = w[:, 4 * row + j : 4 * row + j + 1]
+            if which == 0:
+                nc.scalar.activation(out=dst, in_=src, func=ACT.Copy, scale=wc)
+            else:
+                nc.vector.scalar_tensor_tensor(
+                    out=dst, in0=src, scalar=wc, in1=dst, op0=ALU.mult, op1=ALU.add
+                )
+
+        def merge(s):
+            for k, taps in enumerate(PLANES):
+                if len(taps) > 1:
+                    tap(s, k, 1)
+
+        mem = {}
+
+        def gather(s):
+            half, j = divmod(s, BLOCKS)
+            n, h = divmod(half, 2)
+            for i in (2 * half, 2 * half + 1):
+                if j == 0:
+                    mem[i] = psum.tile([P, C], F32, name="mem", bufs=2)
+                    nc.tensor.matmul(
+                        mem[i][:], ident16[:], sk[n][:, i % 4, :], start=True, stop=False
+                    )
+                cols = slice(P * (i % 4), P * (i % 4) + P)
+                for k in range(len(PLANES)):
+                    nc.tensor.matmul(
+                        mem[i][:, P * j : P * j + P],
+                        y[n, j][:, k, cols],
+                        ident[:],
+                        start=False,
+                        stop=(j == BLOCKS - 1 and k == len(PLANES) - 1),
+                        is_transpose=True,
+                    )
+
+        m16, turned, mg, mq, ms = {}, {}, {}, {}, {}
+
+        def round_m(i):
+            m16[i] = work.tile([P, C], BF16, name="m16", bufs=2)
+            nc.scalar.copy(
+                out=m16[i][:].rearrange("p (u w e) -> p u w e", u=2, e=2),
+                in_=mem[i][:].rearrange("p (w u e) -> p u w e", u=2, e=2),
+            )
+
+        def turn_m(i):
+            words = m16[i][:].bitcast(F32)
+            turned[i] = psum.tile([P, 512], F32, name="turn", bufs=1)
+            for u in range(2):
+                nc.tensor.transpose(
+                    turned[i][:, P * u : P * u + P], words[:, P * u : P * u + P], ident[:]
+                )
+
+        def lay_m(i):
+            mg[i] = work.tile([P, P, 4], BF16, name="mg", bufs=2, align_bytes=64)
+            nc.scalar.copy(
+                out=mg[i][:].rearrange("p r k -> p (r k)").bitcast(F32).rearrange("p (r u) -> p r u", u=2),
+                in_=turned[i][:, 0:256].rearrange("p (u r) -> p r u", u=2),
+            )
+
+        def quantize_m(i):
+            mq[i] = work.tile([P, P], U32, name="mq", bufs=3, align_bytes=64)
+            ms[i] = work.tile([P, P], U8, name="ms", bufs=3, align_bytes=64)
+            nc.vector.quantize_mx(
+                out=mq[i][:].bitcast(FP8X4), scales=ms[i][:], in_=mg[i][:].rearrange("p r k -> p (r k)")
+            )
+
+        acc, o = {}, {}
+
+        def expand(i, f):
+            acc[i, f] = psum.tile([P, 512], F32, name="acc", bufs=2)
+            nc.tensor.matmul_mx(
+                out=acc[i, f][:],
+                lhsT=mq[i][:].bitcast(FP8X4),
+                lhsT_scale=ms[i][:],
+                rhs=uq[:, 512 * f : 512 * f + 512].bitcast(FP8X4),
+                rhs_scale=us[:, 512 * f : 512 * f + 512],
+                start=True,
+                stop=True,
+            )
+
+        def finish(i, f, engine):
+            if f == 0:
+                o[i] = work.tile([P, F], F32, name="o", bufs=4)
+            fc = slice(512 * f, 512 * f + 512)
+            nc.vector.tensor_tensor(out=o[i][:, fc], in0=acc[i, f][:], in1=bias[:, fc], op=ALU.add)
+            if engine == "gpsimd":
+                nc.gpsimd.tensor_scalar(
+                    out=o[i][:, fc], in0=o[i][:, fc], scalar1=BIG, scalar2=0.0, op0=ALU.min, op1=ALU.max
+                )
+            else:
+                nc.scalar.activation(out=o[i][:, fc], in_=o[i][:, fc], func=ACT.Relu)
+            if f % 2 == 1:
+                wide = slice(512 * f - 512, 512 * f + 512)
+                n, k = divmod(i, 4)
+                nc.sync.dma_start(out=out[n, P * k : P * k + P, wide], in_=o[i][:, wide])
+
+        def step(s, row, engine):
+            half, j = divmod(s, BLOCKS)
+            prev = 2 * half - 2
+            later = (prev, prev + 1) if half > 0 else ()
+            if s + 1 < STEPS:
+                project(s + 1)
+            if row is not None:
+                cast(row, engine)
+                turn_x(row, "turn")
+            if s > 0:
+                merge(s - 1)
+            tap(s, 0, 0)
+            tap(s, 1, 0)
+            if j == 1:
+                for i in later:
+                    round_m(i)
+            if j == 2:
+                for i in later:
+                    lay_m(i)
+                    quantize_m(i)
+            tap(s, 2, 0)
+            tap(s, 3, 0)
+            for i, f in pieces(s - 1):
+                finish(i, f, "gpsimd")
+            if row is not None:
+                scale_x(row)
+                quantize_x(row)
+            if s > 0:
+                gather(s - 1)
+            if j == 1:
+                for i in later:
+                    turn_m(i)
+            for i, f in pieces(s):
+                expand(i, f)
+
+        def pieces(s):
+            first = 2 * (s - 6)
+            if first < 0:
+                return ()
+            return tuple(divmod(q, 4) for q in (first, first + 1))
+
+        with tc.manual_schedule():
+            cast(0, "vector")
+            cast(1, "scalar")
+            turn_x(0, "turn")
+            turn_x(1, "acc")
+            scale_x(0)
+            cast(2, "scalar")
+            scale_x(1)
+            quantize_x(0)
+            turn_x(2, "acc")
+            weights()
+            quantize_x(1)
+            scale_x(2)
+            quantize_x(2)
+            project(0)
+            for s in range(STEPS):
+                step(s, *HELP.get(s, (None, None)))
+            merge(STEPS - 1)
+            gather(STEPS - 1)
+            for i, f in pieces(STEPS - 1):
+                finish(i, f, "gpsimd")
+            for i, f in pieces(STEPS):
+                expand(i, f)
+            round_m(6)
+            round_m(7)
+            turn_m(6)
+            turn_m(7)
+            for i, f in pieces(STEPS):
+                finish(i, f, "gpsimd")
+            for i, f in pieces(STEPS + 1):
+                expand(i, f)
+            for i in (6, 7):
+                lay_m(i)
+                quantize_m(i)
+            for s in range(STEPS + 1, STEPS + 6):
+                for q, (i, f) in enumerate(pieces(s)):
+                    finish(i, f, ("gpsimd", "scalar")[q])
+                if s + 1 < STEPS + 6:
+                    for i, f in pieces(s + 1):
+                        expand(i, f)

@@ -22,9 +22,12 @@ STRIDE = 2
 FLOPS = 2 * SEQS * FRAMES * (D * C + C * F)
 BIG = 3.0e38
 
-PLANES = (((0, 0), (1, 2)), ((4, -2), (2, 4)), ((5, -4), (3, 6)), ((6, -6),))
-STEPS = 16
-HELP = {0: (3, "scalar"), 1: (4, "vector"), 2: (5, "scalar"), 3: (6, "vector"), 4: (7, "scalar")}
+VECTOR_TAPS = ((), (((0, 0), (1, 2)), ((2, 4), (4, -2))))
+SCALAR_TAPS = (((0, 0), (1, 2), (2, 4), (4, -2)), ((3, 6), (5, -4), (6, -6)))
+GPSIMD_TAPS = (((3, 6), (5, -4), (6, -6)), ())
+PAD = 6
+VECTOR_CASTS = (0, 1)
+SCALAR_RELU_FROM = 6
 
 
 def tile_deepfsmnstridedmemoryblock_w8_kernel(
@@ -96,45 +99,52 @@ def tile_deepfsmnstridedmemoryblock_w8_kernel(
         make_identity(nc, ident[:])
         ident16 = keep.tile([P, P], BF16, name="ident16")
 
-        y = {}
+        y, ps = {}, {}
         for n in range(SEQS):
             for j in range(BLOCKS):
-                t = keep.tile([P, len(PLANES), FRAMES], F32, name=f"y{n}{j}")
-                for k, taps in enumerate(PLANES):
-                    d = taps[0][1]
-                    if d < 0:
-                        nc.gpsimd.memset(t[:, k, FRAMES + d : FRAMES], 0.0)
-                y[n, j] = t
+                planes = len(VECTOR_TAPS[n]) + len(SCALAR_TAPS[n]) + len(GPSIMD_TAPS[n])
+                y[n, j] = keep.tile([P, planes, FRAMES], F32, name=f"y{n}{j}")
+                for q, pair in enumerate(VECTOR_TAPS[n]):
+                    if pair[0][1] > 0:
+                        nc.gpsimd.memset(y[n, j][:, q, 0 : pair[0][1]], 0.0)
+                ps[n, j] = keep.tile([P, PAD + FRAMES + PAD], F32, name=f"ps{n}{j}")
+                nc.gpsimd.memset(ps[n, j][:, 0:PAD], 0.0)
+                nc.gpsimd.memset(ps[n, j][:, PAD + FRAMES :], 0.0)
 
         w = keep.tile([P, 28], F32, name="w")
         rows32 = keep.tile([P, P], F32, name="rows32")
 
-        def weights():
+        wbank = {}
+
+        def w1():
             nc.vector.tensor_copy(out=rows32[:], in_=rows[:])
-            wt = psum.tile([P, 512], F32, name="turn", bufs=1)
-            nc.tensor.transpose(wt[:, 0:P], rows32[:], ident[:])
-            nc.vector.tensor_copy(out=w[:, 4:28], in_=wt[:, 4:28])
-            nc.vector.tensor_scalar(out=w[:, 0:4], in0=wt[:, 0:4], scalar1=1.0, scalar2=None, op0=ALU.add)
+
+        def w2():
+            wbank[0] = psum.tile([P, 512], F32, name="mem", bufs=2)
+            nc.tensor.transpose(wbank[0][:, 0:P], rows32[:], ident[:])
+
+        def w3():
+            nc.vector.tensor_copy(out=w[:, 4:28], in_=wbank[0][:, 4:28])
+            nc.vector.tensor_scalar(
+                out=w[:, 0:4], in0=wbank[0][:, 0:4], scalar1=1.0, scalar2=None, op0=ALU.add
+            )
             nc.vector.tensor_copy(out=ident16[:], in_=ident[:])
 
-        xq, xqs = {}, {}
-        for n in range(SEQS):
-            xq[n] = keep.tile([P, PASSES, FRAMES], U32, name=f"xq{n}", align_bytes=64)
-            xqs[n] = keep.tile([P, PASSES, FRAMES], U8, name=f"xqs{n}", align_bytes=64)
+        x16, xbank, xg, xq, xqs = {}, {}, {}, {}, {}
 
-        x16, xbank, xg = {}, {}, {}
-
-        def cast(r, engine):
-            x16[r] = work.tile([P, D], BF16, name="x16", bufs=3)
+        def cast(r):
+            engine = "vector" if r in VECTOR_CASTS else "scalar"
+            x16[r] = work.tile([P, D], BF16, name="x16", bufs=8)
             src = xb8[r].bitcast(FP8)
             if engine == "vector":
                 nc.vector.tensor_copy(out=x16[r][:], in_=src)
             else:
                 nc.scalar.copy(out=x16[r][:], in_=src)
 
-        def turn_x(r, tag):
+        def turn_x(r):
+            tag, bufs = (("acc", 3), ("acc", 3), ("acc", 3), ("mem", 2), ("turn", 1), ("turn", 1), ("turn", 1), ("turn", 1))[r]
             words = x16[r][:].bitcast(F32)
-            xbank[r] = psum.tile([P, 512], F32, name=tag, bufs=1 if tag == "turn" else 2)
+            xbank[r] = psum.tile([P, 512], F32, name=tag, bufs=bufs)
             for g in range(PASSES):
                 for u in range(2):
                     nc.tensor.transpose(
@@ -144,10 +154,12 @@ def tile_deepfsmnstridedmemoryblock_w8_kernel(
                     )
 
         def scale_x(r):
-            xg[r] = work.tile([P, PASSES, P, 4], BF16, name="xg", bufs=2, align_bytes=64)
+            pair, k = divmod(r, 2)
+            if pair not in xg:
+                xg[pair] = work.tile([P, PASSES, HALF, 4], BF16, name="xg", bufs=3, align_bytes=64)
             for g in range(PASSES):
                 nc.vector.tensor_tensor(
-                    out=xg[r][:, g, :, :].rearrange("p r (u e) -> p r u e", u=2),
+                    out=xg[pair][:, g, P * k : P * k + P, :].rearrange("p r (u e) -> p r u e", u=2),
                     in0=xbank[r][:, 256 * g : 256 * g + 256]
                     .bitcast(BF16)
                     .rearrange("p (u r e) -> p r u e", u=2, e=2),
@@ -157,79 +169,94 @@ def tile_deepfsmnstridedmemoryblock_w8_kernel(
                     op=ALU.mult,
                 )
 
-        def quantize_x(r):
-            n, i = divmod(r, 4)
-            for g in range(PASSES):
-                nc.vector.quantize_mx(
-                    out=xq[n][:, g, P * i : P * i + P].bitcast(FP8X4),
-                    scales=xqs[n][:, g, P * i : P * i + P],
-                    in_=xg[r][:, g, :, :].rearrange("p r k -> p (r k)"),
-                )
+        def quantize_x(pair):
+            xq[pair] = keep.tile([P, PASSES, HALF], U32, name=f"xq{pair}", align_bytes=64)
+            xqs[pair] = keep.tile([P, PASSES, HALF], U8, name=f"xqs{pair}", align_bytes=64)
+            nc.vector.quantize_mx(
+                out=xq[pair][:].rearrange("p g r -> p (g r)").bitcast(FP8X4),
+                scales=xqs[pair][:].rearrange("p g r -> p (g r)"),
+                in_=xg[pair][:].rearrange("p g r k -> p (g r k)"),
+            )
 
         proj = {}
 
-        def project(s):
-            half, j = divmod(s, BLOCKS)
-            n, h = divmod(half, 2)
-            proj[s] = psum.tile([P, FRAMES], F32, name="proj", bufs=3)
-            for lo, hi in (((0, 256), (256, 384)), ((128, 256), (256, 512)))[h]:
+        def project(n, j):
+            proj[n, j] = psum.tile([P, FRAMES], F32, name="proj", bufs=2)
+            for h in range(2):
+                pair = 2 * n + h
                 for g in range(PASSES):
                     nc.tensor.matmul_mx(
-                        out=proj[s][:, lo:hi],
+                        out=proj[n, j][:, HALF * h : HALF * h + HALF],
                         lhsT=vq[:, g, P * j : P * j + P].bitcast(FP8X4),
                         lhsT_scale=vs[4 * g : P, P * j : P * j + P],
-                        rhs=xq[n][:, g, lo:hi].bitcast(FP8X4),
-                        rhs_scale=xqs[n][:, g, lo:hi],
+                        rhs=xq[pair][:, g, :].bitcast(FP8X4),
+                        rhs_scale=xqs[pair][:, g, :],
                         start=(g == 0),
                         stop=(g == PASSES - 1),
                     )
 
-        def tap(s, plane, which):
-            half, j = divmod(s, BLOCKS)
-            n, h = divmod(half, 2)
-            row, d = PLANES[plane][which]
-            lo, hi = max(HALF * h, d), min(HALF * h + HALF, FRAMES + d)
-            dst = y[n, j][:, plane, lo:hi]
-            src = proj[s][:, lo - d : hi - d]
-            wc = w[:, 4 * row + j : 4 * row + j + 1]
-            if which == 0:
-                nc.scalar.activation(out=dst, in_=src, func=ACT.Copy, scale=wc)
-            else:
-                nc.vector.scalar_tensor_tensor(
-                    out=dst, in0=src, scalar=wc, in1=dst, op0=ALU.mult, op1=ALU.add
-                )
+        def weight(tap, j):
+            return w[:, 4 * tap[0] + j : 4 * tap[0] + j + 1]
 
-        def merge(s):
-            for k, taps in enumerate(PLANES):
-                if len(taps) > 1:
-                    tap(s, k, 1)
+        def keep_p(n, j):
+            nc.scalar.copy(out=ps[n, j][:, PAD : PAD + FRAMES], in_=proj[n, j][:])
+
+        def vector_taps(n, j, q):
+            pair = VECTOR_TAPS[n][q]
+            for k, (row, d) in enumerate(pair):
+                lo, hi = max(0, d), min(FRAMES, FRAMES + d)
+                dst = y[n, j][:, q, lo:hi]
+                src = proj[n, j][:, lo - d : hi - d]
+                if k == 0:
+                    nc.vector.tensor_scalar(
+                        out=dst, in0=src, scalar1=weight((row, d), j), scalar2=None, op0=ALU.mult
+                    )
+                else:
+                    nc.vector.scalar_tensor_tensor(
+                        out=dst, in0=src, scalar=weight((row, d), j), in1=dst, op0=ALU.mult, op1=ALU.add
+                    )
+
+        def plane(h, j, q, tap):
+            n, k = divmod(h, 2)
+            lo = HALF * k
+            return y[n, j][:, q, lo : lo + HALF], ps[n, j][:, PAD + lo - tap[1] : PAD + lo - tap[1] + HALF]
+
+        def scalar_taps(h, j):
+            first = len(VECTOR_TAPS[h // 2])
+            for q, tap in enumerate(SCALAR_TAPS[h // 2]):
+                dst, src = plane(h, j, first + q, tap)
+                nc.scalar.activation(out=dst, in_=src, func=ACT.Copy, scale=weight(tap, j))
+
+        def gpsimd_taps(h, j):
+            first = len(VECTOR_TAPS[h // 2]) + len(SCALAR_TAPS[h // 2])
+            for q, tap in enumerate(GPSIMD_TAPS[h // 2]):
+                dst, src = plane(h, j, first + q, tap)
+                nc.gpsimd.tensor_scalar(
+                    out=dst, in0=src, scalar1=weight(tap, j), scalar2=0.0, op0=ALU.mult, op1=ALU.add
+                )
 
         mem = {}
 
-        def gather(s):
-            half, j = divmod(s, BLOCKS)
-            n, h = divmod(half, 2)
-            for i in (2 * half, 2 * half + 1):
-                if j == 0:
-                    mem[i] = psum.tile([P, C], F32, name="mem", bufs=2)
-                    nc.tensor.matmul(
-                        mem[i][:], ident16[:], sk[n][:, i % 4, :], start=True, stop=False
-                    )
-                cols = slice(P * (i % 4), P * (i % 4) + P)
-                for k in range(len(PLANES)):
-                    nc.tensor.matmul(
-                        mem[i][:, P * j : P * j + P],
-                        y[n, j][:, k, cols],
-                        ident[:],
-                        start=False,
-                        stop=(j == BLOCKS - 1 and k == len(PLANES) - 1),
-                        is_transpose=True,
-                    )
+        def gather(i, j):
+            n, k = divmod(i, 4)
+            planes = y[n, j].shape[1]
+            if j == 0:
+                mem[i] = psum.tile([P, C], F32, name="mem", bufs=2)
+                nc.tensor.matmul(mem[i][:], ident16[:], sk[n][:, k, :], start=True, stop=False)
+            for q in range(planes):
+                nc.tensor.matmul(
+                    mem[i][:, P * j : P * j + P],
+                    y[n, j][:, q, P * k : P * k + P],
+                    ident[:],
+                    start=False,
+                    stop=(j == BLOCKS - 1 and q == planes - 1),
+                    is_transpose=True,
+                )
 
         m16, turned, mg, mq, ms = {}, {}, {}, {}, {}
 
         def round_m(i):
-            m16[i] = work.tile([P, C], BF16, name="m16", bufs=2)
+            m16[i] = work.tile([P, C], BF16, name="m16", bufs=3)
             nc.scalar.copy(
                 out=m16[i][:].rearrange("p (u w e) -> p u w e", u=2, e=2),
                 in_=mem[i][:].rearrange("p (w u e) -> p u w e", u=2, e=2),
@@ -244,15 +271,15 @@ def tile_deepfsmnstridedmemoryblock_w8_kernel(
                 )
 
         def lay_m(i):
-            mg[i] = work.tile([P, P, 4], BF16, name="mg", bufs=2, align_bytes=64)
+            mg[i] = work.tile([P, P, 4], BF16, name="mg", bufs=3, align_bytes=64)
             nc.scalar.copy(
                 out=mg[i][:].rearrange("p r k -> p (r k)").bitcast(F32).rearrange("p (r u) -> p r u", u=2),
                 in_=turned[i][:, 0:256].rearrange("p (u r) -> p r u", u=2),
             )
 
         def quantize_m(i):
-            mq[i] = work.tile([P, P], U32, name="mq", bufs=3, align_bytes=64)
-            ms[i] = work.tile([P, P], U8, name="ms", bufs=3, align_bytes=64)
+            mq[i] = work.tile([P, P], U32, name="mq", bufs=4, align_bytes=64)
+            ms[i] = work.tile([P, P], U8, name="ms", bufs=4, align_bytes=64)
             nc.vector.quantize_mx(
                 out=mq[i][:].bitcast(FP8X4), scales=ms[i][:], in_=mg[i][:].rearrange("p r k -> p (r k)")
             )
@@ -260,7 +287,7 @@ def tile_deepfsmnstridedmemoryblock_w8_kernel(
         acc, o = {}, {}
 
         def expand(i, f):
-            acc[i, f] = psum.tile([P, 512], F32, name="acc", bufs=2)
+            acc[i, f] = psum.tile([P, 512], F32, name="acc", bufs=3)
             nc.tensor.matmul_mx(
                 out=acc[i, f][:],
                 lhsT=mq[i][:].bitcast(FP8X4),
@@ -271,100 +298,266 @@ def tile_deepfsmnstridedmemoryblock_w8_kernel(
                 stop=True,
             )
 
-        def finish(i, f, engine):
-            if f == 0:
+        def finish(i, f):
+            if i not in o:
                 o[i] = work.tile([P, F], F32, name="o", bufs=4)
             fc = slice(512 * f, 512 * f + 512)
             nc.vector.tensor_tensor(out=o[i][:, fc], in0=acc[i, f][:], in1=bias[:, fc], op=ALU.add)
-            if engine == "gpsimd":
+
+        done = set()
+
+        def relu(i, f):
+            fc = slice(512 * f, 512 * f + 512)
+            if i < SCALAR_RELU_FROM or f % 2 == 0:
                 nc.gpsimd.tensor_scalar(
                     out=o[i][:, fc], in0=o[i][:, fc], scalar1=BIG, scalar2=0.0, op0=ALU.min, op1=ALU.max
                 )
             else:
                 nc.scalar.activation(out=o[i][:, fc], in_=o[i][:, fc], func=ACT.Relu)
-            if f % 2 == 1:
+            done.add((i, f))
+            if (i, f ^ 1) in done:
+                f = f | 1
                 wide = slice(512 * f - 512, 512 * f + 512)
                 n, k = divmod(i, 4)
                 nc.sync.dma_start(out=out[n, P * k : P * k + P, wide], in_=o[i][:, wide])
 
-        def step(s, row, engine):
-            half, j = divmod(s, BLOCKS)
-            prev = 2 * half - 2
-            later = (prev, prev + 1) if half > 0 else ()
-            if s + 1 < STEPS:
-                project(s + 1)
-            if row is not None:
-                cast(row, engine)
-                turn_x(row, "turn")
-            if s > 0:
-                merge(s - 1)
-            tap(s, 0, 0)
-            tap(s, 1, 0)
-            if j == 1:
-                for i in later:
-                    round_m(i)
-            if j == 2:
-                for i in later:
-                    lay_m(i)
-                    quantize_m(i)
-            tap(s, 2, 0)
-            tap(s, 3, 0)
-            for i, f in pieces(s - 1):
-                finish(i, f, "gpsimd")
-            if row is not None:
-                scale_x(row)
-                quantize_x(row)
-            if s > 0:
-                gather(s - 1)
-            if j == 1:
-                for i in later:
-                    turn_m(i)
-            for i, f in pieces(s):
-                expand(i, f)
-
-        def pieces(s):
-            first = 2 * (s - 6)
-            if first < 0:
-                return ()
-            return tuple(divmod(q, 4) for q in (first, first + 1))
-
         with tc.manual_schedule():
-            cast(0, "vector")
-            cast(1, "scalar")
-            turn_x(0, "turn")
-            turn_x(1, "acc")
+            cast(0)
+            cast(1)
+            turn_x(0)
+            w1()
+            cast(3)
+            turn_x(1)
             scale_x(0)
-            cast(2, "scalar")
+            w2()
+            cast(2)
+            turn_x(3)
             scale_x(1)
-            quantize_x(0)
-            turn_x(2, "acc")
-            weights()
-            quantize_x(1)
+            turn_x(2)
+            cast(5)
+            scale_x(3)
+            cast(7)
             scale_x(2)
+            turn_x(5)
+            cast(6)
+            quantize_x(0)
+            quantize_x(1)
+            cast(4)
+            scale_x(5)
+            project(0, 0)
+            project(0, 1)
+            w3()
+            keep_p(0, 0)
+            turn_x(7)
+            keep_p(0, 1)
+            gpsimd_taps(0, 0)
+            project(0, 2)
+            scale_x(7)
+            scalar_taps(0, 0)
+            project(0, 3)
+            gpsimd_taps(0, 1)
+            keep_p(0, 2)
+            turn_x(6)
+            gather(0, 0)
+            keep_p(0, 3)
+            scale_x(6)
+            gpsimd_taps(0, 2)
+            scalar_taps(0, 1)
+            gather(1, 0)
+            gpsimd_taps(0, 3)
+            quantize_x(3)
+            turn_x(4)
+            scalar_taps(0, 2)
+            gather(0, 1)
+            scale_x(4)
+            gather(1, 1)
+            gpsimd_taps(1, 0)
+            scalar_taps(0, 3)
+            gather(0, 2)
             quantize_x(2)
-            project(0)
-            for s in range(STEPS):
-                step(s, *HELP.get(s, (None, None)))
-            merge(STEPS - 1)
-            gather(STEPS - 1)
-            for i, f in pieces(STEPS - 1):
-                finish(i, f, "gpsimd")
-            for i, f in pieces(STEPS):
-                expand(i, f)
+            gather(1, 2)
+            gpsimd_taps(1, 1)
+            scalar_taps(1, 0)
+            gather(0, 3)
+            project(1, 0)
+            gpsimd_taps(1, 2)
+            round_m(0)
+            project(1, 1)
+            vector_taps(1, 0, 0)
+            keep_p(1, 0)
+            gather(1, 3)
+            gpsimd_taps(1, 3)
+            keep_p(1, 1)
+            turn_m(0)
+            gather(2, 0)
+            round_m(1)
+            vector_taps(1, 0, 1)
+            lay_m(0)
+            gather(3, 0)
+            scalar_taps(1, 1)
+            quantize_m(0)
+            vector_taps(1, 1, 0)
+            turn_m(1)
+            project(1, 2)
+            scalar_taps(1, 2)
+            expand(0, 0)
+            expand(0, 1)
+            vector_taps(1, 1, 1)
+            expand(0, 2)
+            gather(2, 1)
+            lay_m(1)
+            keep_p(1, 2)
+            gather(2, 2)
+            quantize_m(1)
+            vector_taps(1, 2, 0)
+            scalar_taps(1, 3)
+            project(1, 3)
+            gather(3, 1)
+            vector_taps(1, 2, 1)
+            keep_p(1, 3)
+            gather(3, 2)
+            scalar_taps(2, 0)
+            gather(2, 3)
+            gather(3, 3)
+            vector_taps(1, 3, 0)
+            scalar_taps(2, 1)
+            gather(4, 0)
+            vector_taps(1, 3, 1)
+            gather(5, 0)
+            round_m(2)
+            round_m(3)
+            gather(4, 1)
+            turn_m(2)
+            scalar_taps(2, 2)
+            finish(0, 0)
+            gather(5, 1)
+            finish(0, 1)
+            relu(0, 0)
+            expand(0, 3)
+            lay_m(2)
+            finish(0, 2)
+            gather(4, 2)
+            scalar_taps(2, 3)
+            relu(0, 1)
+            turn_m(3)
+            quantize_m(2)
+            expand(1, 0)
+            finish(0, 3)
+            scalar_taps(3, 0)
+            expand(1, 1)
+            relu(0, 2)
+            gather(4, 3)
+            finish(1, 0)
+            relu(0, 3)
+            expand(1, 2)
+            finish(1, 1)
+            lay_m(3)
+            gather(5, 2)
+            round_m(4)
+            relu(1, 0)
+            finish(1, 2)
+            expand(1, 3)
+            expand(2, 0)
+            scalar_taps(3, 1)
+            relu(1, 1)
+            quantize_m(3)
+            gather(5, 3)
+            finish(1, 3)
+            turn_m(4)
+            relu(1, 2)
+            scalar_taps(3, 2)
+            expand(2, 1)
+            finish(2, 0)
+            expand(2, 2)
+            relu(1, 3)
+            gather(6, 0)
+            finish(2, 1)
+            lay_m(4)
+            relu(2, 0)
+            finish(2, 2)
+            round_m(5)
+            expand(2, 3)
+            expand(3, 0)
+            quantize_m(4)
+            scalar_taps(3, 3)
+            relu(2, 1)
+            gather(6, 1)
+            finish(2, 3)
+            turn_m(5)
+            relu(2, 2)
+            finish(3, 0)
+            expand(3, 1)
+            expand(3, 2)
+            lay_m(5)
+            relu(2, 3)
+            gather(6, 2)
+            finish(3, 1)
+            expand(3, 3)
+            quantize_m(5)
+            relu(3, 0)
+            gather(6, 3)
+            finish(3, 2)
+            expand(4, 0)
+            relu(3, 1)
+            finish(3, 3)
+            gather(7, 0)
             round_m(6)
-            round_m(7)
+            finish(4, 0)
+            relu(3, 2)
+            expand(4, 1)
             turn_m(6)
+            relu(3, 3)
+            expand(4, 2)
+            finish(4, 1)
+            expand(4, 3)
+            lay_m(6)
+            relu(4, 0)
+            gather(7, 1)
+            finish(4, 2)
+            expand(5, 0)
+            quantize_m(6)
+            relu(4, 1)
+            gather(7, 2)
+            finish(4, 3)
+            expand(5, 1)
+            relu(4, 2)
+            finish(5, 0)
+            gather(7, 3)
+            expand(5, 2)
+            finish(5, 1)
+            relu(4, 3)
+            expand(5, 3)
+            round_m(7)
+            finish(5, 2)
+            relu(5, 0)
+            expand(6, 0)
             turn_m(7)
-            for i, f in pieces(STEPS):
-                finish(i, f, "gpsimd")
-            for i, f in pieces(STEPS + 1):
-                expand(i, f)
-            for i in (6, 7):
-                lay_m(i)
-                quantize_m(i)
-            for s in range(STEPS + 1, STEPS + 6):
-                for q, (i, f) in enumerate(pieces(s)):
-                    finish(i, f, ("gpsimd", "scalar")[q])
-                if s + 1 < STEPS + 6:
-                    for i, f in pieces(s + 1):
-                        expand(i, f)
+            finish(5, 3)
+            relu(5, 1)
+            expand(6, 1)
+            finish(6, 0)
+            lay_m(7)
+            relu(5, 2)
+            expand(6, 2)
+            finish(6, 1)
+            expand(6, 3)
+            relu(5, 3)
+            quantize_m(7)
+            finish(6, 2)
+            relu(6, 1)
+            relu(6, 0)
+            expand(7, 0)
+            finish(6, 3)
+            expand(7, 1)
+            relu(6, 2)
+            finish(7, 0)
+            relu(6, 3)
+            expand(7, 2)
+            finish(7, 1)
+            relu(7, 0)
+            expand(7, 3)
+            finish(7, 2)
+            relu(7, 1)
+            finish(7, 3)
+            relu(7, 2)
+            relu(7, 3)

@@ -22,12 +22,12 @@ STRIDE = 2
 FLOPS = 2 * SEQS * FRAMES * (D * C + C * F)
 BIG = 3.0e38
 
-VECTOR_TAPS = ((), (((0, 0), (1, 2)), ((2, 4), (4, -2))))
-SCALAR_TAPS = (((0, 0), (1, 2), (2, 4), (4, -2)), ((3, 6), (5, -4), (6, -6)))
-GPSIMD_TAPS = (((3, 6), (5, -4), (6, -6)), ())
+MERGED_TAPS = ((), (((0, 0), (1, 2)),))
+PLANE_TAPS = (((0, 0), (1, 2), (2, 4), (3, 6), (4, -2), (5, -4), (6, -6)), ((2, 4), (3, 6), (4, -2), (5, -4), (6, -6)))
+WIDTH = (256, 256)
 PAD = 6
-VECTOR_CASTS = (0, 1)
-SCALAR_RELU_FROM = 6
+BANKS = {'proj': 2, 'mem': 2, 'acc': 3, 'turn': 1}
+SPARE = (1, 3)
 
 
 def tile_deepfsmnstridedmemoryblock_w8_kernel(
@@ -51,17 +51,18 @@ def tile_deepfsmnstridedmemoryblock_w8_kernel(
                 xb8[4 * n + first + r] = t[:, r, :]
 
         load_x(0, 0, 1)
-        xs = keep.tile([P, PASSES, 4], F32, name="xs")
-        with nc.allow_non_contiguous_dma(reason="16-byte runs of the input scales"):
-            nc.sync.dma_start(
-                out=xs[:], in_=x_scale.rearrange("o q (g p t) -> p (o q g) t", p=P, t=4)
+        xs = keep.tile([P, D], F32, name="xs")
+        for g in range(PASSES):
+            k = slice(512 * g, 512 * g + 512)
+            nc.scalar.dma_start(
+                out=xs[:, k], in_=x_scale.rearrange("o q k -> (o q k)")[k].partition_broadcast(P)
             )
+        load_x(0, 1, 1)
+        load_x(0, 2, 2)
         rows = keep.tile([P, P], BF16, name="rows")
         nc.vector.memset(rows[:], 0.0)
         nc.sync.dma_start(out=rows[0:16, :], in_=a.rearrange("s (j q) -> (s j) q", q=P))
         nc.sync.dma_start(out=rows[16:28, :], in_=c.rearrange("s (j q) -> (s j) q", q=P))
-        load_x(0, 1, 1)
-        load_x(0, 2, 2)
         vq = keep.tile([P, PASSES, C], U32, name="vq", align_bytes=64)
         nc.sync.dma_start(
             out=vq[:].bitcast(I32),
@@ -98,13 +99,17 @@ def tile_deepfsmnstridedmemoryblock_w8_kernel(
         ident = keep.tile([P, P], F32, name="ident")
         make_identity(nc, ident[:])
         ident16 = keep.tile([P, P], BF16, name="ident16")
+        nc.gpsimd.tensor_copy(out=ident16[:], in_=ident[:])
+        one = keep.tile([P, 28], F32, name="one")
+        nc.gpsimd.memset(one[:], 0.0)
+        nc.gpsimd.memset(one[:, 0:BLOCKS], 1.0)
 
         y, ps = {}, {}
         for n in range(SEQS):
             for j in range(BLOCKS):
-                planes = len(VECTOR_TAPS[n]) + len(SCALAR_TAPS[n]) + len(GPSIMD_TAPS[n])
+                planes = len(MERGED_TAPS[n]) + len(PLANE_TAPS[n])
                 y[n, j] = keep.tile([P, planes, FRAMES], F32, name=f"y{n}{j}")
-                for q, pair in enumerate(VECTOR_TAPS[n]):
+                for q, pair in enumerate(MERGED_TAPS[n]):
                     if pair[0][1] > 0:
                         nc.gpsimd.memset(y[n, j][:, q, 0 : pair[0][1]], 0.0)
                 ps[n, j] = keep.tile([P, PAD + FRAMES + PAD], F32, name=f"ps{n}{j}")
@@ -112,37 +117,21 @@ def tile_deepfsmnstridedmemoryblock_w8_kernel(
                 nc.gpsimd.memset(ps[n, j][:, PAD + FRAMES :], 0.0)
 
         w = keep.tile([P, 28], F32, name="w")
-        rows32 = keep.tile([P, P], F32, name="rows32")
-
         wbank = {}
 
-        def w1():
-            nc.vector.tensor_copy(out=rows32[:], in_=rows[:])
-
         def w2():
-            wbank[0] = psum.tile([P, 512], F32, name="mem", bufs=2)
-            nc.tensor.transpose(wbank[0][:, 0:P], rows32[:], ident[:])
+            wbank[0] = psum.tile([P, 512], F32, name="mem", bufs=BANKS["mem"])
+            nc.tensor.transpose(wbank[0][:].bitcast(BF16)[:, 0:P], rows[:], ident16[:])
 
         def w3():
-            nc.vector.tensor_copy(out=w[:, 4:28], in_=wbank[0][:, 4:28])
-            nc.vector.tensor_scalar(
-                out=w[:, 0:4], in0=wbank[0][:, 0:4], scalar1=1.0, scalar2=None, op0=ALU.add
+            nc.vector.tensor_tensor(
+                out=w[:], in0=wbank[0][:].bitcast(BF16)[:, 0:28], in1=one[:], op=ALU.add
             )
-            nc.vector.tensor_copy(out=ident16[:], in_=ident[:])
 
         x16, xbank, xg, xq, xqs = {}, {}, {}, {}, {}
 
-        def cast(r):
-            engine = "vector" if r in VECTOR_CASTS else "scalar"
-            x16[r] = work.tile([P, D], BF16, name="x16", bufs=8)
-            src = xb8[r].bitcast(FP8)
-            if engine == "vector":
-                nc.vector.tensor_copy(out=x16[r][:], in_=src)
-            else:
-                nc.scalar.copy(out=x16[r][:], in_=src)
-
         def turn_x(r):
-            tag, bufs = (("acc", 3), ("acc", 3), ("acc", 3), ("mem", 2), ("turn", 1), ("turn", 1), ("turn", 1), ("turn", 1))[r]
+            tag, bufs = (("acc", 3), ("acc", 3), ("acc", 3), ("mem", 2), ("acc", 3), ("acc", 3), ("acc", 3), ("turn", 1))[r]
             words = x16[r][:].bitcast(F32)
             xbank[r] = psum.tile([P, 512], F32, name=tag, bufs=bufs)
             for g in range(PASSES):
@@ -153,21 +142,29 @@ def tile_deepfsmnstridedmemoryblock_w8_kernel(
                         ident[:],
                     )
 
-        def scale_x(r):
+        def scale_x(r, lo=0, hi=D):
+            if r not in x16:
+                x16[r] = work.tile([P, D], BF16, name="x16", bufs=4)
+            nc.vector.tensor_tensor(
+                out=x16[r][:, lo:hi], in0=xb8[r][:, lo:hi].bitcast(FP8), in1=xs[:, lo:hi], op=ALU.mult
+            )
+
+        def copy(engine, out, in_):
+            if engine == "vector":
+                nc.vector.tensor_copy(out=out, in_=in_)
+            else:
+                nc.scalar.copy(out=out, in_=in_)
+
+        def lay_x(r, engine):
             pair, k = divmod(r, 2)
             if pair not in xg:
                 xg[pair] = work.tile([P, PASSES, HALF, 4], BF16, name="xg", bufs=3, align_bytes=64)
-            for g in range(PASSES):
-                nc.vector.tensor_tensor(
-                    out=xg[pair][:, g, P * k : P * k + P, :].rearrange("p r (u e) -> p r u e", u=2),
-                    in0=xbank[r][:, 256 * g : 256 * g + 256]
-                    .bitcast(BF16)
-                    .rearrange("p (u r e) -> p r u e", u=2, e=2),
-                    in1=xs[:, g, :]
-                    .rearrange("p (o u e) -> p o u e", o=1, u=2)
-                    .to_broadcast([P, P, 2, 2]),
-                    op=ALU.mult,
-                )
+            copy(
+                engine,
+                xg[pair][:].rearrange("p g r k -> p (g r k)").bitcast(F32)
+                .rearrange("p (g r u) -> p g r u", g=PASSES, u=2)[:, :, P * k : P * k + P, :],
+                xbank[r][:].rearrange("p (g u r) -> p g r u", g=PASSES, u=2),
+            )
 
         def quantize_x(pair):
             xq[pair] = keep.tile([P, PASSES, HALF], U32, name=f"xq{pair}", align_bytes=64)
@@ -181,7 +178,7 @@ def tile_deepfsmnstridedmemoryblock_w8_kernel(
         proj = {}
 
         def project(n, j):
-            proj[n, j] = psum.tile([P, FRAMES], F32, name="proj", bufs=2)
+            proj[n, j] = psum.tile([P, FRAMES], F32, name="proj", bufs=BANKS["proj"])
             for h in range(2):
                 pair = 2 * n + h
                 for g in range(PASSES):
@@ -198,11 +195,11 @@ def tile_deepfsmnstridedmemoryblock_w8_kernel(
         def weight(tap, j):
             return w[:, 4 * tap[0] + j : 4 * tap[0] + j + 1]
 
-        def keep_p(n, j):
-            nc.scalar.copy(out=ps[n, j][:, PAD : PAD + FRAMES], in_=proj[n, j][:])
+        def keep_p(n, j, engine):
+            copy(engine, ps[n, j][:, PAD : PAD + FRAMES], proj[n, j][:])
 
-        def vector_taps(n, j, q):
-            pair = VECTOR_TAPS[n][q]
+        def merged_taps(n, j, q):
+            pair = MERGED_TAPS[n][q]
             for k, (row, d) in enumerate(pair):
                 lo, hi = max(0, d), min(FRAMES, FRAMES + d)
                 dst = y[n, j][:, q, lo:hi]
@@ -216,33 +213,30 @@ def tile_deepfsmnstridedmemoryblock_w8_kernel(
                         out=dst, in0=src, scalar=weight((row, d), j), in1=dst, op0=ALU.mult, op1=ALU.add
                     )
 
-        def plane(h, j, q, tap):
-            n, k = divmod(h, 2)
-            lo = HALF * k
-            return y[n, j][:, q, lo : lo + HALF], ps[n, j][:, PAD + lo - tap[1] : PAD + lo - tap[1] + HALF]
-
-        def scalar_taps(h, j):
-            first = len(VECTOR_TAPS[h // 2])
-            for q, tap in enumerate(SCALAR_TAPS[h // 2]):
-                dst, src = plane(h, j, first + q, tap)
+        def plane_tap(n, part, j, q, engine):
+            tap, width = PLANE_TAPS[n][q], WIDTH[n]
+            lo = width * part
+            dst = y[n, j][:, len(MERGED_TAPS[n]) + q, lo : lo + width]
+            src = ps[n, j][:, PAD + lo - tap[1] : PAD + lo - tap[1] + width]
+            if engine == "scalar":
                 nc.scalar.activation(out=dst, in_=src, func=ACT.Copy, scale=weight(tap, j))
-
-        def gpsimd_taps(h, j):
-            first = len(VECTOR_TAPS[h // 2]) + len(SCALAR_TAPS[h // 2])
-            for q, tap in enumerate(GPSIMD_TAPS[h // 2]):
-                dst, src = plane(h, j, first + q, tap)
+            elif engine == "vector":
+                nc.vector.tensor_scalar(out=dst, in0=src, scalar1=weight(tap, j), scalar2=None, op0=ALU.mult)
+            else:
                 nc.gpsimd.tensor_scalar(
                     out=dst, in0=src, scalar1=weight(tap, j), scalar2=0.0, op0=ALU.mult, op1=ALU.add
                 )
 
         mem = {}
 
+        def open_mem(i):
+            n, k = divmod(i, 4)
+            mem[i] = psum.tile([P, C], F32, name="mem", bufs=BANKS["mem"])
+            nc.tensor.matmul(mem[i][:], ident16[:], sk[n][:, k, :], start=True, stop=False)
+
         def gather(i, j):
             n, k = divmod(i, 4)
             planes = y[n, j].shape[1]
-            if j == 0:
-                mem[i] = psum.tile([P, C], F32, name="mem", bufs=2)
-                nc.tensor.matmul(mem[i][:], ident16[:], sk[n][:, k, :], start=True, stop=False)
             for q in range(planes):
                 nc.tensor.matmul(
                     mem[i][:, P * j : P * j + P],
@@ -255,26 +249,28 @@ def tile_deepfsmnstridedmemoryblock_w8_kernel(
 
         m16, turned, mg, mq, ms = {}, {}, {}, {}, {}
 
-        def round_m(i):
+        def round_m(i, engine):
             m16[i] = work.tile([P, C], BF16, name="m16", bufs=3)
-            nc.scalar.copy(
-                out=m16[i][:].rearrange("p (u w e) -> p u w e", u=2, e=2),
-                in_=mem[i][:].rearrange("p (w u e) -> p u w e", u=2, e=2),
+            copy(
+                engine,
+                m16[i][:].rearrange("p (u w e) -> p u w e", u=2, e=2),
+                mem[i][:].rearrange("p (w u e) -> p u w e", u=2, e=2),
             )
 
         def turn_m(i):
             words = m16[i][:].bitcast(F32)
-            turned[i] = psum.tile([P, 512], F32, name="turn", bufs=1)
+            turned[i] = psum.tile([P, 512], F32, name="turn", bufs=BANKS["turn"])
             for u in range(2):
                 nc.tensor.transpose(
                     turned[i][:, P * u : P * u + P], words[:, P * u : P * u + P], ident[:]
                 )
 
-        def lay_m(i):
+        def lay_m(i, engine):
             mg[i] = work.tile([P, P, 4], BF16, name="mg", bufs=3, align_bytes=64)
-            nc.scalar.copy(
-                out=mg[i][:].rearrange("p r k -> p (r k)").bitcast(F32).rearrange("p (r u) -> p r u", u=2),
-                in_=turned[i][:, 0:256].rearrange("p (u r) -> p r u", u=2),
+            copy(
+                engine,
+                mg[i][:].rearrange("p r k -> p (r k)").bitcast(F32).rearrange("p (r u) -> p r u", u=2),
+                turned[i][:, 0:256].rearrange("p (u r) -> p r u", u=2),
             )
 
         def quantize_m(i):
@@ -287,7 +283,8 @@ def tile_deepfsmnstridedmemoryblock_w8_kernel(
         acc, o = {}, {}
 
         def expand(i, f):
-            acc[i, f] = psum.tile([P, 512], F32, name="acc", bufs=3)
+            tag = "proj" if 4 * i + f >= 4 and (4 * i + f) % 5 in SPARE else "acc"
+            acc[i, f] = psum.tile([P, 512], F32, name=tag, bufs=BANKS[tag])
             nc.tensor.matmul_mx(
                 out=acc[i, f][:],
                 lhsT=mq[i][:].bitcast(FP8X4),
@@ -300,264 +297,345 @@ def tile_deepfsmnstridedmemoryblock_w8_kernel(
 
         def finish(i, f):
             if i not in o:
-                o[i] = work.tile([P, F], F32, name="o", bufs=4)
+                o[i] = work.tile([P, F], F32, name="o", bufs=5)
             fc = slice(512 * f, 512 * f + 512)
             nc.vector.tensor_tensor(out=o[i][:, fc], in0=acc[i, f][:], in1=bias[:, fc], op=ALU.add)
 
-        done = set()
-
-        def relu(i, f):
-            fc = slice(512 * f, 512 * f + 512)
-            if i < SCALAR_RELU_FROM or f % 2 == 0:
-                nc.gpsimd.tensor_scalar(
-                    out=o[i][:, fc], in0=o[i][:, fc], scalar1=BIG, scalar2=0.0, op0=ALU.min, op1=ALU.max
-                )
+        def relu(i, lo, hi, engine):
+            piece = o[i][:, lo:hi]
+            if engine == "scalar":
+                nc.scalar.activation(out=piece, in_=piece, func=ACT.Relu)
+            elif engine == "vector":
+                nc.vector.tensor_scalar(out=piece, in0=piece, scalar1=0.0, scalar2=None, op0=ALU.max)
             else:
-                nc.scalar.activation(out=o[i][:, fc], in_=o[i][:, fc], func=ACT.Relu)
-            done.add((i, f))
-            if (i, f ^ 1) in done:
-                f = f | 1
-                wide = slice(512 * f - 512, 512 * f + 512)
-                n, k = divmod(i, 4)
-                nc.sync.dma_start(out=out[n, P * k : P * k + P, wide], in_=o[i][:, wide])
+                nc.gpsimd.tensor_scalar(out=piece, in0=piece, scalar1=BIG, scalar2=0.0, op0=ALU.min, op1=ALU.max)
+
+        def store(i, lo, hi):
+            n, k = divmod(i, 4)
+            wide = slice(lo, hi)
+            nc.sync.dma_start(out=out[n, P * k : P * k + P, wide], in_=o[i][:, wide])
 
         with tc.manual_schedule():
-            cast(0)
-            cast(1)
-            turn_x(0)
-            w1()
-            cast(3)
-            turn_x(1)
-            scale_x(0)
-            w2()
-            cast(2)
-            turn_x(3)
+            scale_x(0, 0, 512)
             scale_x(1)
-            turn_x(2)
-            cast(5)
-            scale_x(3)
-            cast(7)
+            turn_x(1)
+            scale_x(0, 512, 1024)
+            lay_x(1, "scalar")
+            turn_x(0)
+            lay_x(0, "scalar")
             scale_x(2)
-            turn_x(5)
-            cast(6)
+            turn_x(2)
+            lay_x(2, "scalar")
+            w2()
+            scale_x(3)
+            turn_x(3)
+            lay_x(3, "scalar")
             quantize_x(0)
-            quantize_x(1)
-            cast(4)
-            scale_x(5)
-            project(0, 0)
-            project(0, 1)
-            w3()
-            keep_p(0, 0)
-            turn_x(7)
-            keep_p(0, 1)
-            gpsimd_taps(0, 0)
-            project(0, 2)
             scale_x(7)
-            scalar_taps(0, 0)
-            project(0, 3)
-            gpsimd_taps(0, 1)
-            keep_p(0, 2)
-            turn_x(6)
-            gather(0, 0)
-            keep_p(0, 3)
+            turn_x(7)
+            lay_x(7, "scalar")
+            w3()
+            open_mem(0)
+            quantize_x(1)
             scale_x(6)
-            gpsimd_taps(0, 2)
-            scalar_taps(0, 1)
-            gather(1, 0)
-            gpsimd_taps(0, 3)
-            quantize_x(3)
-            turn_x(4)
-            scalar_taps(0, 2)
-            gather(0, 1)
+            project(0, 0)
+            keep_p(0, 0, "scalar")
             scale_x(4)
-            gather(1, 1)
-            gpsimd_taps(1, 0)
-            scalar_taps(0, 3)
-            gather(0, 2)
+            plane_tap(0, 0, 0, 0, "vector")
+            project(0, 3)
+            keep_p(0, 3, "scalar")
+            turn_x(6)
+            plane_tap(0, 0, 0, 4, "scalar")
+            project(0, 2)
+            project(0, 1)
+            plane_tap(0, 0, 0, 6, "vector")
+            scale_x(5)
+            lay_x(6, "scalar")
+            plane_tap(0, 0, 0, 1, "vector")
+            quantize_x(3)
+            keep_p(0, 2, "scalar")
+            plane_tap(0, 0, 2, 6, "vector")
+            keep_p(0, 1, "scalar")
+            plane_tap(0, 0, 1, 1, "vector")
+            turn_x(4)
+            lay_x(4, "scalar")
+            plane_tap(0, 0, 1, 0, "vector")
+            plane_tap(0, 0, 2, 5, "vector")
+            turn_x(5)
+            lay_x(5, "scalar")
+            plane_tap(0, 0, 1, 4, "scalar")
+            plane_tap(0, 0, 2, 4, "scalar")
+            plane_tap(0, 0, 2, 2, "scalar")
+            plane_tap(0, 0, 3, 0, "vector")
+            plane_tap(0, 0, 0, 5, "vector")
+            plane_tap(0, 0, 1, 2, "scalar")
+            open_mem(1)
+            plane_tap(0, 0, 3, 4, "scalar")
             quantize_x(2)
-            gather(1, 2)
-            gpsimd_taps(1, 1)
-            scalar_taps(1, 0)
-            gather(0, 3)
+            plane_tap(0, 0, 0, 2, "scalar")
+            plane_tap(0, 1, 1, 5, "scalar")
             project(1, 0)
-            gpsimd_taps(1, 2)
-            round_m(0)
+            plane_tap(0, 0, 1, 6, "vector")
+            plane_tap(0, 1, 1, 3, "scalar")
+            plane_tap(0, 0, 2, 0, "vector")
+            plane_tap(0, 1, 0, 6, "vector")
+            plane_tap(0, 1, 0, 3, "scalar")
+            plane_tap(0, 0, 0, 3, "vector")
+            plane_tap(0, 0, 1, 3, "vector")
             project(1, 1)
-            vector_taps(1, 0, 0)
-            keep_p(1, 0)
-            gather(1, 3)
-            gpsimd_taps(1, 3)
-            keep_p(1, 1)
+            plane_tap(0, 0, 3, 6, "vector")
+            plane_tap(0, 0, 2, 3, "vector")
+            plane_tap(0, 1, 0, 1, "scalar")
+            plane_tap(0, 0, 1, 5, "vector")
+            plane_tap(0, 1, 0, 0, "vector")
+            plane_tap(0, 0, 2, 1, "vector")
+            plane_tap(0, 0, 3, 1, "vector")
+            plane_tap(0, 0, 3, 2, "scalar")
+            plane_tap(0, 0, 3, 3, "vector")
+            gather(0, 0)
+            plane_tap(0, 0, 3, 5, "vector")
+            plane_tap(0, 1, 0, 4, "vector")
+            plane_tap(0, 1, 1, 4, "vector")
+            plane_tap(0, 1, 0, 5, "scalar")
+            plane_tap(0, 1, 1, 1, "scalar")
+            keep_p(1, 0, "scalar")
+            gather(0, 1)
+            gather(0, 2)
+            gather(0, 3)
+            plane_tap(0, 1, 0, 2, "vector")
+            round_m(0, "scalar")
+            plane_tap(0, 1, 1, 2, "vector")
+            plane_tap(0, 1, 1, 6, "vector")
+            plane_tap(0, 1, 1, 0, "vector")
+            keep_p(1, 1, "scalar")
+            plane_tap(0, 1, 2, 6, "vector")
+            plane_tap(0, 1, 3, 5, "scalar")
+            plane_tap(1, 0, 0, 0, "gpsimd")
+            merged_taps(1, 0, 0)
+            plane_tap(0, 1, 2, 5, "scalar")
+            merged_taps(1, 1, 0)
+            gather(1, 0)
+            gather(1, 1)
+            plane_tap(1, 0, 0, 1, "gpsimd")
             turn_m(0)
+            plane_tap(1, 1, 0, 3, "gpsimd")
+            plane_tap(1, 1, 1, 3, "gpsimd")
+            plane_tap(0, 1, 3, 1, "scalar")
+            open_mem(2)
+            plane_tap(1, 0, 1, 0, "gpsimd")
             gather(2, 0)
-            round_m(1)
-            vector_taps(1, 0, 1)
-            lay_m(0)
-            gather(3, 0)
-            scalar_taps(1, 1)
-            quantize_m(0)
-            vector_taps(1, 1, 0)
-            turn_m(1)
-            project(1, 2)
-            scalar_taps(1, 2)
-            expand(0, 0)
-            expand(0, 1)
-            vector_taps(1, 1, 1)
-            expand(0, 2)
+            plane_tap(0, 1, 2, 4, "vector")
             gather(2, 1)
-            lay_m(1)
-            keep_p(1, 2)
-            gather(2, 2)
-            quantize_m(1)
-            vector_taps(1, 2, 0)
-            scalar_taps(1, 3)
+            plane_tap(0, 1, 2, 1, "scalar")
+            lay_m(0, "scalar")
+            quantize_m(0)
+            plane_tap(0, 1, 2, 0, "vector")
+            plane_tap(0, 1, 2, 3, "scalar")
+            plane_tap(0, 1, 3, 3, "scalar")
             project(1, 3)
-            gather(3, 1)
-            vector_taps(1, 2, 1)
-            keep_p(1, 3)
-            gather(3, 2)
-            scalar_taps(2, 0)
-            gather(2, 3)
-            gather(3, 3)
-            vector_taps(1, 3, 0)
-            scalar_taps(2, 1)
-            gather(4, 0)
-            vector_taps(1, 3, 1)
-            gather(5, 0)
-            round_m(2)
-            round_m(3)
-            gather(4, 1)
-            turn_m(2)
-            scalar_taps(2, 2)
-            finish(0, 0)
-            gather(5, 1)
+            plane_tap(0, 1, 2, 2, "vector")
+            plane_tap(0, 1, 3, 2, "vector")
+            plane_tap(1, 0, 0, 3, "scalar")
+            plane_tap(0, 1, 3, 6, "vector")
+            plane_tap(0, 1, 3, 0, "vector")
+            plane_tap(0, 1, 3, 4, "vector")
+            plane_tap(1, 1, 0, 1, "vector")
+            project(1, 2)
+            keep_p(1, 2, "scalar")
+            plane_tap(1, 0, 2, 0, "gpsimd")
+            plane_tap(1, 1, 2, 0, "gpsimd")
+            expand(0, 1)
             finish(0, 1)
-            relu(0, 0)
             expand(0, 3)
-            lay_m(2)
-            finish(0, 2)
-            gather(4, 2)
-            scalar_taps(2, 3)
-            relu(0, 1)
-            turn_m(3)
-            quantize_m(2)
-            expand(1, 0)
+            keep_p(1, 3, "scalar")
+            plane_tap(1, 0, 3, 1, "gpsimd")
+            expand(0, 0)
+            finish(0, 0)
+            plane_tap(1, 0, 1, 1, "gpsimd")
+            plane_tap(1, 0, 3, 4, "scalar")
+            gather(1, 2)
+            plane_tap(1, 0, 3, 3, "scalar")
+            gather(1, 3)
+            plane_tap(1, 1, 1, 2, "gpsimd")
+            plane_tap(1, 1, 0, 0, "gpsimd")
+            gather(2, 2)
+            round_m(1, "scalar")
+            plane_tap(1, 1, 3, 4, "scalar")
+            plane_tap(1, 1, 0, 4, "scalar")
+            gather(2, 3)
+            round_m(2, "scalar")
+            merged_taps(1, 3, 0)
             finish(0, 3)
-            scalar_taps(3, 0)
-            expand(1, 1)
-            relu(0, 2)
-            gather(4, 3)
-            finish(1, 0)
-            relu(0, 3)
+            expand(0, 2)
+            open_mem(3)
+            finish(0, 2)
+            turn_m(1)
+            lay_m(1, "scalar")
+            gather(3, 0)
+            gather(3, 1)
+            plane_tap(1, 0, 2, 3, "scalar")
+            plane_tap(1, 0, 0, 2, "scalar")
+            plane_tap(1, 1, 2, 1, "vector")
+            plane_tap(1, 0, 2, 4, "scalar")
+            turn_m(2)
+            lay_m(2, "scalar")
+            gather(3, 2)
+            gather(3, 3)
+            quantize_m(1)
+            plane_tap(1, 0, 1, 2, "scalar")
+            plane_tap(1, 0, 2, 2, "scalar")
+            expand(1, 0)
+            round_m(3, "scalar")
+            plane_tap(1, 0, 1, 4, "scalar")
+            plane_tap(1, 1, 0, 2, "gpsimd")
+            plane_tap(1, 1, 2, 2, "gpsimd")
+            merged_taps(1, 2, 0)
+            open_mem(4)
+            quantize_m(2)
             expand(1, 2)
-            finish(1, 1)
-            lay_m(3)
-            gather(5, 2)
-            round_m(4)
-            relu(1, 0)
-            finish(1, 2)
-            expand(1, 3)
-            expand(2, 0)
-            scalar_taps(3, 1)
-            relu(1, 1)
-            quantize_m(3)
-            gather(5, 3)
-            finish(1, 3)
-            turn_m(4)
-            relu(1, 2)
-            scalar_taps(3, 2)
+            plane_tap(1, 1, 1, 1, "vector")
+            finish(1, 0)
+            plane_tap(1, 0, 3, 2, "scalar")
             expand(2, 1)
-            finish(2, 0)
-            expand(2, 2)
-            relu(1, 3)
-            gather(6, 0)
+            plane_tap(1, 0, 0, 4, "scalar")
             finish(2, 1)
-            lay_m(4)
-            relu(2, 0)
-            finish(2, 2)
-            round_m(5)
+            plane_tap(1, 0, 1, 3, "scalar")
+            expand(1, 1)
+            finish(1, 1)
             expand(2, 3)
-            expand(3, 0)
-            quantize_m(4)
-            scalar_taps(3, 3)
-            relu(2, 1)
-            gather(6, 1)
+            open_mem(5)
             finish(2, 3)
-            turn_m(5)
-            relu(2, 2)
-            finish(3, 0)
-            expand(3, 1)
+            plane_tap(1, 1, 3, 2, "gpsimd")
+            plane_tap(1, 1, 2, 4, "scalar")
+            expand(2, 2)
+            plane_tap(1, 0, 2, 1, "gpsimd")
+            plane_tap(1, 1, 1, 0, "gpsimd")
+            plane_tap(1, 0, 3, 0, "gpsimd")
+            turn_m(3)
+            lay_m(3, "scalar")
+            finish(1, 2)
+            gather(4, 0)
+            gather(4, 1)
+            relu(0, 1024, 2048, "scalar")
+            plane_tap(1, 1, 1, 4, "scalar")
+            gather(4, 2)
+            gather(4, 3)
+            plane_tap(1, 1, 3, 3, "gpsimd")
+            expand(1, 3)
+            quantize_m(3)
+            round_m(4, "scalar")
+            finish(2, 2)
+            relu(2, 1024, 2048, "scalar")
+            relu(0, 0, 1024, "vector")
             expand(3, 2)
-            lay_m(5)
-            relu(2, 3)
-            gather(6, 2)
+            finish(1, 3)
+            store(0, 1024, 2048)
+            store(0, 0, 1024)
+            plane_tap(1, 1, 2, 3, "gpsimd")
+            plane_tap(1, 1, 3, 1, "vector")
+            expand(2, 0)
+            expand(3, 1)
+            finish(2, 0)
+            expand(3, 0)
+            turn_m(4)
+            finish(3, 0)
+            plane_tap(1, 1, 3, 0, "gpsimd")
+            gather(5, 0)
+            gather(5, 1)
+            relu(1, 1024, 2048, "gpsimd")
+            gather(5, 2)
+            gather(5, 3)
             finish(3, 1)
             expand(3, 3)
-            quantize_m(5)
-            relu(3, 0)
-            gather(6, 3)
-            finish(3, 2)
+            lay_m(4, "scalar")
+            store(2, 1024, 2048)
+            open_mem(6)
+            relu(1, 0, 1024, "scalar")
+            quantize_m(4)
             expand(4, 0)
-            relu(3, 1)
-            finish(3, 3)
-            gather(7, 0)
-            round_m(6)
-            finish(4, 0)
-            relu(3, 2)
-            expand(4, 1)
-            turn_m(6)
-            relu(3, 3)
             expand(4, 2)
-            finish(4, 1)
+            finish(3, 2)
+            relu(2, 0, 1024, "gpsimd")
             expand(4, 3)
-            lay_m(6)
-            relu(4, 0)
-            gather(7, 1)
+            store(1, 0, 1024)
+            store(1, 1024, 2048)
+            round_m(5, "scalar")
+            finish(3, 3)
+            relu(3, 0, 1024, "scalar")
+            store(3, 0, 1024)
+            expand(4, 1)
+            relu(3, 1024, 2048, "gpsimd")
+            turn_m(5)
+            lay_m(5, "scalar")
             finish(4, 2)
-            expand(5, 0)
-            quantize_m(6)
-            relu(4, 1)
-            gather(7, 2)
             finish(4, 3)
-            expand(5, 1)
-            relu(4, 2)
-            finish(5, 0)
-            gather(7, 3)
+            store(3, 1024, 2048)
+            store(2, 0, 1024)
+            finish(4, 0)
+            gather(6, 0)
+            gather(6, 1)
+            gather(6, 2)
+            gather(6, 3)
+            quantize_m(5)
             expand(5, 2)
-            finish(5, 1)
-            relu(4, 3)
-            expand(5, 3)
-            round_m(7)
+            finish(4, 1)
+            relu(4, 1024, 2048, "scalar")
+            open_mem(7)
             finish(5, 2)
-            relu(5, 0)
-            expand(6, 0)
-            turn_m(7)
-            finish(5, 3)
-            relu(5, 1)
-            expand(6, 1)
-            finish(6, 0)
-            lay_m(7)
-            relu(5, 2)
-            expand(6, 2)
-            finish(6, 1)
+            relu(5, 1024, 1536, "gpsimd")
+            expand(5, 0)
+            finish(5, 0)
+            expand(5, 3)
+            expand(5, 1)
+            round_m(6, "scalar")
+            turn_m(6)
+            finish(5, 1)
+            gather(7, 0)
+            gather(7, 1)
+            relu(4, 0, 1024, "scalar")
+            gather(7, 2)
+            gather(7, 3)
+            lay_m(6, "scalar")
+            store(4, 1024, 2048)
+            quantize_m(6)
             expand(6, 3)
-            relu(5, 3)
-            quantize_m(7)
-            finish(6, 2)
-            relu(6, 1)
-            relu(6, 0)
-            expand(7, 0)
+            round_m(7, "scalar")
+            store(4, 0, 1024)
+            relu(5, 0, 1024, "vector")
+            store(5, 0, 1024)
+            expand(6, 1)
+            finish(5, 3)
+            relu(5, 1536, 2048, "scalar")
             finish(6, 3)
-            expand(7, 1)
-            relu(6, 2)
-            finish(7, 0)
-            relu(6, 3)
+            expand(6, 0)
+            finish(6, 0)
+            store(5, 1024, 2048)
+            finish(6, 1)
+            turn_m(7)
+            lay_m(7, "scalar")
+            expand(6, 2)
+            relu(6, 1536, 2048, "gpsimd")
+            store(6, 1536, 2048)
+            quantize_m(7)
+            relu(6, 0, 512, "scalar")
             expand(7, 2)
-            finish(7, 1)
-            relu(7, 0)
             expand(7, 3)
+            relu(6, 512, 1024, "scalar")
+            store(6, 0, 1024)
+            finish(6, 2)
+            relu(6, 1024, 1536, "scalar")
+            expand(7, 1)
             finish(7, 2)
-            relu(7, 1)
+            store(6, 1024, 1536)
+            relu(7, 1024, 1536, "scalar")
+            store(7, 1024, 1536)
             finish(7, 3)
-            relu(7, 2)
-            relu(7, 3)
+            relu(7, 1536, 2048, "scalar")
+            finish(7, 1)
+            expand(7, 0)
+            store(7, 1536, 2048)
+            finish(7, 0)
+            relu(7, 512, 1024, "scalar")
+            relu(7, 0, 512, "vector")
+            store(7, 512, 1024)
+            store(7, 0, 512)

@@ -51,13 +51,12 @@ def tile_deepfsmnstridedmemoryblock_w8_kernel(
                 xb8[4 * n + first + r] = t[:, r, :]
 
         load_x(0, 0, 1)
-        xs = keep.tile([P, D], F32, name="xs")
-        for g in range(PASSES):
-            k = slice(512 * g, 512 * g + 512)
-            nc.scalar.dma_start(
-                out=xs[:, k], in_=x_scale.rearrange("o q k -> (o q k)")[k].partition_broadcast(P)
-            )
         load_x(0, 1, 1)
+        xs = keep.tile([P, PASSES, 4], F32, name="xs")
+        with nc.allow_non_contiguous_dma(reason="16-byte runs of the input scales"):
+            nc.sync.dma_start(
+                out=xs[:], in_=x_scale.rearrange("o q (g p t) -> p (o q g) t", p=P, t=4)
+            )
         load_x(0, 2, 2)
         rows = keep.tile([P, P], BF16, name="rows")
         nc.vector.memset(rows[:], 0.0)
@@ -131,7 +130,7 @@ def tile_deepfsmnstridedmemoryblock_w8_kernel(
         x16, xbank, xg, xq, xqs = {}, {}, {}, {}, {}
 
         def turn_x(r):
-            tag, bufs = (("acc", 3), ("acc", 3), ("acc", 3), ("mem", 2), ("acc", 3), ("acc", 3), ("acc", 3), ("turn", 1))[r]
+            tag, bufs = (("acc", 3), ("acc", 3), ("acc", 3), ("mem", 2), ("turn", 1), ("acc", 3), ("acc", 3), ("acc", 3))[r]
             words = x16[r][:].bitcast(F32)
             xbank[r] = psum.tile([P, 512], F32, name=tag, bufs=bufs)
             for g in range(PASSES):
@@ -142,29 +141,31 @@ def tile_deepfsmnstridedmemoryblock_w8_kernel(
                         ident[:],
                     )
 
-        def scale_x(r, lo=0, hi=D):
-            if r not in x16:
-                x16[r] = work.tile([P, D], BF16, name="x16", bufs=4)
-            nc.vector.tensor_tensor(
-                out=x16[r][:, lo:hi], in0=xb8[r][:, lo:hi].bitcast(FP8), in1=xs[:, lo:hi], op=ALU.mult
-            )
-
         def copy(engine, out, in_):
             if engine == "vector":
                 nc.vector.tensor_copy(out=out, in_=in_)
             else:
                 nc.scalar.copy(out=out, in_=in_)
 
-        def lay_x(r, engine):
+        def cast(r, engine):
+            x16[r] = work.tile([P, D], BF16, name="x16", bufs=5)
+            copy(engine, x16[r][:], xb8[r].bitcast(FP8))
+
+        def scale_x(r):
             pair, k = divmod(r, 2)
             if pair not in xg:
                 xg[pair] = work.tile([P, PASSES, HALF, 4], BF16, name="xg", bufs=3, align_bytes=64)
-            copy(
-                engine,
-                xg[pair][:].rearrange("p g r k -> p (g r k)").bitcast(F32)
-                .rearrange("p (g r u) -> p g r u", g=PASSES, u=2)[:, :, P * k : P * k + P, :],
-                xbank[r][:].rearrange("p (g u r) -> p g r u", g=PASSES, u=2),
-            )
+            for g in range(PASSES):
+                nc.vector.tensor_tensor(
+                    out=xg[pair][:, g, P * k : P * k + P, :].rearrange("p r (u e) -> p r u e", u=2),
+                    in0=xbank[r][:, 256 * g : 256 * g + 256]
+                    .bitcast(BF16)
+                    .rearrange("p (u r e) -> p r u e", u=2, e=2),
+                    in1=xs[:, g, :]
+                    .rearrange("p (o u e) -> p o u e", o=1, u=2)
+                    .to_broadcast([P, P, 2, 2]),
+                    op=ALU.mult,
+                )
 
         def quantize_x(pair):
             xq[pair] = keep.tile([P, PASSES, HALF], U32, name=f"xq{pair}", align_bytes=64)
@@ -295,11 +296,13 @@ def tile_deepfsmnstridedmemoryblock_w8_kernel(
                 stop=True,
             )
 
-        def finish(i, f):
+        def finish(i, lo, hi):
             if i not in o:
                 o[i] = work.tile([P, F], F32, name="o", bufs=5)
-            fc = slice(512 * f, 512 * f + 512)
-            nc.vector.tensor_tensor(out=o[i][:, fc], in0=acc[i, f][:], in1=bias[:, fc], op=ALU.add)
+            f, at = divmod(lo, 512)
+            nc.vector.tensor_tensor(
+                out=o[i][:, lo:hi], in0=acc[i, f][:, at : at + hi - lo], in1=bias[:, lo:hi], op=ALU.add
+            )
 
         def relu(i, lo, hi, engine):
             piece = o[i][:, lo:hi]
@@ -316,326 +319,328 @@ def tile_deepfsmnstridedmemoryblock_w8_kernel(
             nc.sync.dma_start(out=out[n, P * k : P * k + P, wide], in_=o[i][:, wide])
 
         with tc.manual_schedule():
-            scale_x(0, 0, 512)
-            scale_x(1)
-            turn_x(1)
-            scale_x(0, 512, 1024)
-            lay_x(1, "scalar")
+            cast(0, "vector")
             turn_x(0)
-            lay_x(0, "scalar")
-            scale_x(2)
-            turn_x(2)
-            lay_x(2, "scalar")
-            w2()
-            scale_x(3)
+            scale_x(0)
+            cast(1, "scalar")
+            turn_x(1)
+            scale_x(1)
+            cast(3, "scalar")
+            cast(2, "scalar")
             turn_x(3)
-            lay_x(3, "scalar")
+            scale_x(3)
+            turn_x(2)
+            scale_x(2)
             quantize_x(0)
-            scale_x(7)
-            turn_x(7)
-            lay_x(7, "scalar")
+            w2()
             w3()
-            open_mem(0)
-            quantize_x(1)
-            scale_x(6)
-            project(0, 0)
-            keep_p(0, 0, "scalar")
-            scale_x(4)
-            plane_tap(0, 0, 0, 0, "vector")
-            project(0, 3)
-            keep_p(0, 3, "scalar")
-            turn_x(6)
-            plane_tap(0, 0, 0, 4, "scalar")
-            project(0, 2)
-            project(0, 1)
-            plane_tap(0, 0, 0, 6, "vector")
-            scale_x(5)
-            lay_x(6, "scalar")
-            plane_tap(0, 0, 0, 1, "vector")
-            quantize_x(3)
-            keep_p(0, 2, "scalar")
-            plane_tap(0, 0, 2, 6, "vector")
-            keep_p(0, 1, "scalar")
-            plane_tap(0, 0, 1, 1, "vector")
+            cast(4, "scalar")
             turn_x(4)
-            lay_x(4, "scalar")
-            plane_tap(0, 0, 1, 0, "vector")
-            plane_tap(0, 0, 2, 5, "vector")
+            cast(5, "scalar")
             turn_x(5)
-            lay_x(5, "scalar")
-            plane_tap(0, 0, 1, 4, "scalar")
-            plane_tap(0, 0, 2, 4, "scalar")
-            plane_tap(0, 0, 2, 2, "scalar")
-            plane_tap(0, 0, 3, 0, "vector")
-            plane_tap(0, 0, 0, 5, "vector")
-            plane_tap(0, 0, 1, 2, "scalar")
-            open_mem(1)
-            plane_tap(0, 0, 3, 4, "scalar")
-            quantize_x(2)
-            plane_tap(0, 0, 0, 2, "scalar")
-            plane_tap(0, 1, 1, 5, "scalar")
-            project(1, 0)
+            open_mem(0)
+            cast(6, "scalar")
+            quantize_x(1)
+            project(0, 1)
+            scale_x(4)
+            project(0, 3)
+            scale_x(5)
+            cast(7, "scalar")
+            turn_x(7)
+            keep_p(0, 1, "scalar")
+            plane_tap(0, 1, 1, 1, "vector")
             plane_tap(0, 0, 1, 6, "vector")
-            plane_tap(0, 1, 1, 3, "scalar")
-            plane_tap(0, 0, 2, 0, "vector")
-            plane_tap(0, 1, 0, 6, "vector")
-            plane_tap(0, 1, 0, 3, "scalar")
-            plane_tap(0, 0, 0, 3, "vector")
-            plane_tap(0, 0, 1, 3, "vector")
-            project(1, 1)
-            plane_tap(0, 0, 3, 6, "vector")
-            plane_tap(0, 0, 2, 3, "vector")
-            plane_tap(0, 1, 0, 1, "scalar")
-            plane_tap(0, 0, 1, 5, "vector")
-            plane_tap(0, 1, 0, 0, "vector")
-            plane_tap(0, 0, 2, 1, "vector")
-            plane_tap(0, 0, 3, 1, "vector")
+            project(0, 0)
+            scale_x(7)
+            open_mem(1)
+            plane_tap(0, 0, 1, 0, "gpsimd")
+            keep_p(0, 3, "scalar")
+            plane_tap(0, 0, 3, 0, "gpsimd")
+            plane_tap(0, 0, 1, 2, "scalar")
+            plane_tap(0, 0, 1, 4, "scalar")
+            project(0, 2)
+            quantize_x(2)
+            plane_tap(0, 0, 1, 3, "scalar")
+            turn_x(6)
+            scale_x(6)
+            keep_p(0, 0, "scalar")
+            plane_tap(0, 0, 0, 0, "gpsimd")
+            keep_p(0, 2, "scalar")
+            plane_tap(0, 0, 2, 0, "gpsimd")
             plane_tap(0, 0, 3, 2, "scalar")
-            plane_tap(0, 0, 3, 3, "vector")
+            plane_tap(0, 0, 1, 5, "vector")
+            quantize_x(3)
+            project(1, 3)
+            plane_tap(0, 0, 2, 2, "scalar")
+            plane_tap(0, 0, 0, 1, "scalar")
+            plane_tap(0, 0, 2, 5, "vector")
+            plane_tap(0, 0, 3, 1, "scalar")
+            plane_tap(0, 0, 2, 6, "vector")
+            project(1, 0)
+            plane_tap(0, 1, 0, 3, "vector")
+            plane_tap(0, 0, 0, 2, "scalar")
+            plane_tap(0, 0, 0, 5, "vector")
+            plane_tap(0, 0, 2, 1, "scalar")
+            plane_tap(0, 0, 0, 6, "vector")
+            plane_tap(0, 0, 0, 3, "scalar")
+            plane_tap(0, 0, 1, 1, "scalar")
+            plane_tap(0, 0, 0, 4, "scalar")
+            plane_tap(0, 1, 0, 5, "vector")
+            plane_tap(0, 1, 0, 0, "vector")
             gather(0, 0)
+            plane_tap(0, 0, 2, 4, "scalar")
             plane_tap(0, 0, 3, 5, "vector")
-            plane_tap(0, 1, 0, 4, "vector")
-            plane_tap(0, 1, 1, 4, "vector")
-            plane_tap(0, 1, 0, 5, "scalar")
-            plane_tap(0, 1, 1, 1, "scalar")
-            keep_p(1, 0, "scalar")
             gather(0, 1)
-            gather(0, 2)
-            gather(0, 3)
             plane_tap(0, 1, 0, 2, "vector")
-            round_m(0, "scalar")
-            plane_tap(0, 1, 1, 2, "vector")
+            plane_tap(0, 0, 3, 6, "vector")
+            plane_tap(0, 1, 0, 1, "vector")
+            plane_tap(0, 1, 0, 6, "vector")
+            keep_p(1, 3, "scalar")
+            plane_tap(1, 1, 3, 1, "gpsimd")
+            merged_taps(1, 3, 0)
             plane_tap(0, 1, 1, 6, "vector")
             plane_tap(0, 1, 1, 0, "vector")
-            keep_p(1, 1, "scalar")
-            plane_tap(0, 1, 2, 6, "vector")
-            plane_tap(0, 1, 3, 5, "scalar")
-            plane_tap(1, 0, 0, 0, "gpsimd")
-            merged_taps(1, 0, 0)
-            plane_tap(0, 1, 2, 5, "scalar")
-            merged_taps(1, 1, 0)
-            gather(1, 0)
-            gather(1, 1)
-            plane_tap(1, 0, 0, 1, "gpsimd")
-            turn_m(0)
-            plane_tap(1, 1, 0, 3, "gpsimd")
-            plane_tap(1, 1, 1, 3, "gpsimd")
-            plane_tap(0, 1, 3, 1, "scalar")
-            open_mem(2)
-            plane_tap(1, 0, 1, 0, "gpsimd")
-            gather(2, 0)
-            plane_tap(0, 1, 2, 4, "vector")
-            gather(2, 1)
-            plane_tap(0, 1, 2, 1, "scalar")
-            lay_m(0, "scalar")
-            quantize_m(0)
+            plane_tap(0, 0, 2, 3, "scalar")
             plane_tap(0, 1, 2, 0, "vector")
-            plane_tap(0, 1, 2, 3, "scalar")
-            plane_tap(0, 1, 3, 3, "scalar")
-            project(1, 3)
+            plane_tap(0, 1, 2, 3, "vector")
+            plane_tap(0, 1, 1, 3, "vector")
+            plane_tap(0, 0, 3, 3, "scalar")
+            plane_tap(0, 0, 3, 4, "scalar")
+            gather(0, 2)
+            gather(0, 3)
+            plane_tap(0, 1, 2, 5, "vector")
+            plane_tap(0, 1, 1, 5, "vector")
+            plane_tap(0, 1, 0, 4, "scalar")
+            gather(1, 0)
+            project(1, 2)
+            keep_p(1, 0, "scalar")
+            round_m(0, "scalar")
+            open_mem(2)
+            gather(2, 0)
+            plane_tap(0, 1, 2, 4, "scalar")
+            plane_tap(0, 1, 1, 2, "vector")
+            plane_tap(0, 1, 1, 4, "scalar")
+            plane_tap(0, 1, 3, 4, "scalar")
+            plane_tap(1, 0, 0, 1, "scalar")
+            plane_tap(0, 1, 2, 6, "vector")
             plane_tap(0, 1, 2, 2, "vector")
             plane_tap(0, 1, 3, 2, "vector")
-            plane_tap(1, 0, 0, 3, "scalar")
+            plane_tap(0, 1, 2, 1, "vector")
+            turn_m(0)
+            plane_tap(0, 1, 3, 5, "vector")
+            keep_p(1, 2, "scalar")
+            plane_tap(0, 1, 3, 3, "vector")
+            lay_m(0, "scalar")
             plane_tap(0, 1, 3, 6, "vector")
             plane_tap(0, 1, 3, 0, "vector")
-            plane_tap(0, 1, 3, 4, "vector")
-            plane_tap(1, 1, 0, 1, "vector")
-            project(1, 2)
-            keep_p(1, 2, "scalar")
-            plane_tap(1, 0, 2, 0, "gpsimd")
-            plane_tap(1, 1, 2, 0, "gpsimd")
-            expand(0, 1)
-            finish(0, 1)
-            expand(0, 3)
-            keep_p(1, 3, "scalar")
-            plane_tap(1, 0, 3, 1, "gpsimd")
-            expand(0, 0)
-            finish(0, 0)
-            plane_tap(1, 0, 1, 1, "gpsimd")
-            plane_tap(1, 0, 3, 4, "scalar")
-            gather(1, 2)
-            plane_tap(1, 0, 3, 3, "scalar")
-            gather(1, 3)
-            plane_tap(1, 1, 1, 2, "gpsimd")
-            plane_tap(1, 1, 0, 0, "gpsimd")
+            gather(1, 1)
+            gather(2, 1)
             gather(2, 2)
-            round_m(1, "scalar")
-            plane_tap(1, 1, 3, 4, "scalar")
-            plane_tap(1, 1, 0, 4, "scalar")
+            quantize_m(0)
+            plane_tap(1, 0, 0, 3, "scalar")
+            gather(1, 2)
+            plane_tap(1, 0, 2, 3, "scalar")
+            plane_tap(0, 1, 3, 1, "vector")
+            gather(1, 3)
+            merged_taps(1, 0, 0)
+            merged_taps(1, 2, 0)
+            plane_tap(1, 0, 3, 1, "scalar")
             gather(2, 3)
-            round_m(2, "scalar")
-            merged_taps(1, 3, 0)
-            finish(0, 3)
-            expand(0, 2)
+            expand(0, 3)
+            plane_tap(1, 0, 3, 2, "gpsimd")
+            plane_tap(1, 0, 3, 4, "scalar")
+            plane_tap(1, 0, 3, 0, "scalar")
+            expand(0, 1)
+            plane_tap(1, 0, 2, 0, "scalar")
+            round_m(1, "scalar")
+            plane_tap(1, 1, 0, 0, "gpsimd")
+            plane_tap(1, 0, 0, 2, "gpsimd")
+            plane_tap(1, 0, 0, 4, "scalar")
+            plane_tap(1, 1, 2, 4, "scalar")
+            project(1, 1)
+            expand(0, 0)
             open_mem(3)
-            finish(0, 2)
             turn_m(1)
-            lay_m(1, "scalar")
+            round_m(2, "scalar")
+            plane_tap(1, 1, 3, 2, "gpsimd")
+            keep_p(1, 1, "scalar")
+            plane_tap(1, 1, 2, 1, "gpsimd")
             gather(3, 0)
             gather(3, 1)
-            plane_tap(1, 0, 2, 3, "scalar")
-            plane_tap(1, 0, 0, 2, "scalar")
-            plane_tap(1, 1, 2, 1, "vector")
-            plane_tap(1, 0, 2, 4, "scalar")
+            lay_m(1, "scalar")
             turn_m(2)
-            lay_m(2, "scalar")
+            plane_tap(1, 1, 0, 1, "gpsimd")
+            finish(0, 512, 1024)
+            plane_tap(1, 0, 1, 0, "scalar")
+            plane_tap(1, 1, 3, 0, "gpsimd")
+            finish(0, 1536, 2048)
             gather(3, 2)
             gather(3, 3)
-            quantize_m(1)
-            plane_tap(1, 0, 1, 2, "scalar")
-            plane_tap(1, 0, 2, 2, "scalar")
-            expand(1, 0)
-            round_m(3, "scalar")
-            plane_tap(1, 0, 1, 4, "scalar")
-            plane_tap(1, 1, 0, 2, "gpsimd")
-            plane_tap(1, 1, 2, 2, "gpsimd")
-            merged_taps(1, 2, 0)
-            open_mem(4)
-            quantize_m(2)
-            expand(1, 2)
-            plane_tap(1, 1, 1, 1, "vector")
-            finish(1, 0)
-            plane_tap(1, 0, 3, 2, "scalar")
-            expand(2, 1)
-            plane_tap(1, 0, 0, 4, "scalar")
-            finish(2, 1)
+            plane_tap(1, 0, 0, 0, "scalar")
             plane_tap(1, 0, 1, 3, "scalar")
-            expand(1, 1)
-            finish(1, 1)
-            expand(2, 3)
-            open_mem(5)
-            finish(2, 3)
-            plane_tap(1, 1, 3, 2, "gpsimd")
-            plane_tap(1, 1, 2, 4, "scalar")
-            expand(2, 2)
-            plane_tap(1, 0, 2, 1, "gpsimd")
-            plane_tap(1, 1, 1, 0, "gpsimd")
-            plane_tap(1, 0, 3, 0, "gpsimd")
-            turn_m(3)
-            lay_m(3, "scalar")
-            finish(1, 2)
-            gather(4, 0)
-            gather(4, 1)
-            relu(0, 1024, 2048, "scalar")
-            plane_tap(1, 1, 1, 4, "scalar")
-            gather(4, 2)
-            gather(4, 3)
-            plane_tap(1, 1, 3, 3, "gpsimd")
-            expand(1, 3)
-            quantize_m(3)
-            round_m(4, "scalar")
-            finish(2, 2)
-            relu(2, 1024, 2048, "scalar")
-            relu(0, 0, 1024, "vector")
-            expand(3, 2)
-            finish(1, 3)
-            store(0, 1024, 2048)
-            store(0, 0, 1024)
-            plane_tap(1, 1, 2, 3, "gpsimd")
-            plane_tap(1, 1, 3, 1, "vector")
+            expand(0, 2)
+            plane_tap(1, 1, 1, 1, "gpsimd")
+            finish(0, 0, 512)
+            lay_m(2, "scalar")
+            merged_taps(1, 1, 0)
+            plane_tap(1, 1, 1, 3, "gpsimd")
+            relu(0, 0, 1024, "scalar")
+            open_mem(4)
+            plane_tap(1, 1, 2, 2, "gpsimd")
+            quantize_m(2)
             expand(2, 0)
-            expand(3, 1)
-            finish(2, 0)
-            expand(3, 0)
-            turn_m(4)
-            finish(3, 0)
-            plane_tap(1, 1, 3, 0, "gpsimd")
-            gather(5, 0)
-            gather(5, 1)
-            relu(1, 1024, 2048, "gpsimd")
-            gather(5, 2)
-            gather(5, 3)
-            finish(3, 1)
-            expand(3, 3)
-            lay_m(4, "scalar")
-            store(2, 1024, 2048)
-            open_mem(6)
-            relu(1, 0, 1024, "scalar")
-            quantize_m(4)
-            expand(4, 0)
-            expand(4, 2)
-            finish(3, 2)
-            relu(2, 0, 1024, "gpsimd")
-            expand(4, 3)
-            store(1, 0, 1024)
+            quantize_m(1)
+            expand(1, 3)
+            expand(2, 1)
+            plane_tap(1, 0, 2, 2, "gpsimd")
+            round_m(3, "scalar")
+            finish(0, 1024, 1536)
+            expand(1, 2)
+            expand(1, 1)
+            plane_tap(1, 0, 1, 1, "scalar")
+            turn_m(3)
+            finish(2, 0, 512)
+            plane_tap(1, 1, 0, 3, "gpsimd")
+            plane_tap(1, 0, 1, 2, "gpsimd")
+            plane_tap(1, 1, 2, 3, "gpsimd")
+            plane_tap(1, 1, 0, 2, "gpsimd")
+            gather(4, 0)
+            finish(2, 512, 1024)
+            plane_tap(1, 0, 1, 4, "scalar")
+            gather(4, 1)
+            plane_tap(1, 0, 2, 4, "scalar")
+            plane_tap(1, 0, 2, 1, "scalar")
+            gather(4, 2)
+            plane_tap(1, 0, 3, 3, "scalar")
+            gather(4, 3)
+            store(0, 0, 1024)
+            finish(1, 512, 1024)
+            lay_m(3, "scalar")
+            finish(1, 1536, 2048)
+            plane_tap(1, 1, 1, 2, "gpsimd")
+            quantize_m(3)
+            expand(2, 3)
+            expand(1, 0)
+            relu(0, 1024, 2048, "scalar")
+            plane_tap(1, 1, 1, 0, "gpsimd")
+            expand(3, 2)
+            store(0, 1024, 2048)
+            finish(1, 1024, 1536)
+            relu(1, 1024, 2048, "vector")
             store(1, 1024, 2048)
+            finish(3, 1024, 1536)
+            finish(1, 0, 512)
+            open_mem(5)
+            plane_tap(1, 1, 2, 0, "gpsimd")
+            expand(3, 3)
+            expand(3, 1)
+            round_m(4, "scalar")
+            plane_tap(1, 1, 0, 4, "scalar")
+            turn_m(4)
+            finish(3, 512, 1024)
+            plane_tap(1, 1, 3, 4, "scalar")
+            gather(5, 0)
+            plane_tap(1, 1, 1, 4, "scalar")
+            gather(5, 1)
+            gather(5, 2)
+            plane_tap(1, 1, 3, 3, "gpsimd")
+            lay_m(4, "scalar")
+            gather(5, 3)
+            quantize_m(4)
+            relu(2, 0, 1024, "scalar")
+            finish(2, 1536, 2048)
+            store(2, 0, 1024)
+            expand(2, 2)
+            expand(3, 0)
+            finish(3, 1536, 2048)
+            finish(2, 1024, 1536)
+            expand(4, 2)
+            finish(4, 1024, 1536)
+            open_mem(6)
+            expand(4, 0)
+            finish(4, 0, 512)
+            relu(1, 0, 1024, "scalar")
+            store(1, 0, 1024)
             round_m(5, "scalar")
-            finish(3, 3)
-            relu(3, 0, 1024, "scalar")
-            store(3, 0, 1024)
+            expand(4, 3)
             expand(4, 1)
-            relu(3, 1024, 2048, "gpsimd")
+            finish(4, 512, 1024)
+            finish(3, 0, 512)
+            relu(2, 1024, 2048, "scalar")
             turn_m(5)
             lay_m(5, "scalar")
-            finish(4, 2)
-            finish(4, 3)
-            store(3, 1024, 2048)
-            store(2, 0, 1024)
-            finish(4, 0)
+            relu(4, 0, 1024, "scalar")
             gather(6, 0)
+            relu(3, 1024, 2048, "gpsimd")
             gather(6, 1)
             gather(6, 2)
             gather(6, 3)
-            quantize_m(5)
-            expand(5, 2)
-            finish(4, 1)
-            relu(4, 1024, 2048, "scalar")
             open_mem(7)
-            finish(5, 2)
-            relu(5, 1024, 1536, "gpsimd")
-            expand(5, 0)
-            finish(5, 0)
+            quantize_m(5)
             expand(5, 3)
+            expand(5, 2)
+            store(3, 1024, 2048)
+            finish(4, 1536, 2048)
+            relu(3, 0, 1024, "gpsimd")
             expand(5, 1)
+            expand(5, 0)
             round_m(6, "scalar")
             turn_m(6)
-            finish(5, 1)
+            lay_m(6, "scalar")
+            finish(5, 1536, 2048)
+            finish(5, 1024, 1536)
+            finish(5, 0, 512)
+            relu(4, 1024, 2048, "gpsimd")
+            quantize_m(6)
             gather(7, 0)
             gather(7, 1)
-            relu(4, 0, 1024, "scalar")
             gather(7, 2)
             gather(7, 3)
-            lay_m(6, "scalar")
-            store(4, 1024, 2048)
-            quantize_m(6)
-            expand(6, 3)
-            round_m(7, "scalar")
+            finish(5, 512, 1024)
+            relu(5, 0, 1024, "gpsimd")
+            store(2, 1024, 2048)
             store(4, 0, 1024)
-            relu(5, 0, 1024, "vector")
-            store(5, 0, 1024)
-            expand(6, 1)
-            finish(5, 3)
             relu(5, 1536, 2048, "scalar")
-            finish(6, 3)
+            expand(6, 3)
+            finish(6, 1536, 2048)
+            relu(6, 1536, 2048, "gpsimd")
+            store(3, 0, 1024)
             expand(6, 0)
-            finish(6, 0)
+            store(4, 1024, 2048)
+            expand(6, 2)
+            relu(5, 1024, 1536, "scalar")
             store(5, 1024, 2048)
-            finish(6, 1)
+            round_m(7, "scalar")
             turn_m(7)
             lay_m(7, "scalar")
-            expand(6, 2)
-            relu(6, 1536, 2048, "gpsimd")
-            store(6, 1536, 2048)
-            quantize_m(7)
+            finish(6, 1024, 1536)
+            relu(6, 1024, 1536, "scalar")
+            finish(6, 0, 512)
             relu(6, 0, 512, "scalar")
-            expand(7, 2)
-            expand(7, 3)
+            quantize_m(7)
+            store(5, 0, 1024)
+            store(6, 1024, 1536)
+            store(6, 1536, 2048)
+            expand(6, 1)
+            finish(6, 512, 1024)
             relu(6, 512, 1024, "scalar")
             store(6, 0, 1024)
-            finish(6, 2)
-            relu(6, 1024, 1536, "scalar")
+            expand(7, 3)
+            finish(7, 1792, 2048)
             expand(7, 1)
-            finish(7, 2)
-            store(6, 1024, 1536)
-            relu(7, 1024, 1536, "scalar")
-            store(7, 1024, 1536)
-            finish(7, 3)
-            relu(7, 1536, 2048, "scalar")
-            finish(7, 1)
-            expand(7, 0)
-            store(7, 1536, 2048)
-            finish(7, 0)
+            relu(7, 1792, 2048, "gpsimd")
+            store(7, 1792, 2048)
+            finish(7, 512, 1024)
             relu(7, 512, 1024, "scalar")
-            relu(7, 0, 512, "vector")
+            expand(7, 2)
+            expand(7, 0)
+            finish(7, 1024, 1536)
+            finish(7, 1536, 1792)
+            relu(7, 1024, 1536, "vector")
             store(7, 512, 1024)
+            store(7, 1024, 1536)
+            finish(7, 0, 512)
+            relu(7, 1536, 1792, "scalar")
+            store(7, 1536, 1792)
+            relu(7, 0, 512, "vector")
             store(7, 0, 512)

from contextlib import ExitStack

import concourse.mybir as mybir
from concourse.masks import make_identity

F32 = mybir.dt.float32
BF16 = mybir.dt.bfloat16
I32 = mybir.dt.int32
U32 = mybir.dt.uint32
U8 = mybir.dt.uint8
FP8 = mybir.dt.float8_e4m3fn
FP8X4 = mybir.dt.float8_e4m3fn_x4
ALU = mybir.AluOpType
ACT = mybir.ActivationFunctionType

P = 128
SEQS, FRAMES, D, C, F = 2, 512, 1024, 512, 2048
HALF = 256
BLOCKS = C // P
PASSES = D // 512
STRIDE = 2
FLOPS = 2 * SEQS * FRAMES * (D * C + C * F)
BIG = 3.0e38

MERGED_TAPS = ((), (((0, 0), (1, 2)),))
PLANE_TAPS = (((0, 0), (1, 2), (2, 4), (3, 6), (4, -2), (5, -4), (6, -6)), ((2, 4), (3, 6), (4, -2), (5, -4), (6, -6)))
WIDTH = (256, 256)
PAD = 6
BANKS = {'proj': 2, 'mem': 2, 'acc': 3, 'turn': 1}
SPARE = (1, 3)


def tile_deepfsmnstridedmemoryblock_w8_kernel(
    tc, x_bytes, x_scale, skip, v_words, v_scales, a, c, u_words, u_scales, b, out
):
    nc = tc.nc
    with ExitStack() as ctx:
        keep = ctx.enter_context(tc.tile_pool(name="keep", bufs=1))
        work = ctx.enter_context(tc.tile_pool(name="work", bufs=3))
        psum = ctx.enter_context(tc.psum_pool(name="psum", bufs=1))

        xb8 = {}

        def load_x(n, first, count):
            t = keep.tile([P, count, D], U8, name=f"xbytes{n}{first}")
            nc.sync.dma_start(
                out=t[:],
                in_=x_bytes[n, P * first : P * (first + count), :].rearrange("(r p) k -> p r k", p=P),
            )
            for r in range(count):
                xb8[4 * n + first + r] = t[:, r, :]

        load_x(0, 0, 1)
        load_x(0, 1, 1)
        xs = keep.tile([P, PASSES, 4], F32, name="xs")
        with nc.allow_non_contiguous_dma(reason="16-byte runs of the input scales"):
            nc.sync.dma_start(
                out=xs[:], in_=x_scale.rearrange("o q (g p t) -> p (o q g) t", p=P, t=4)
            )
        load_x(0, 2, 2)
        rows = keep.tile([P, P], BF16, name="rows")
        nc.vector.memset(rows[:], 0.0)
        nc.sync.dma_start(out=rows[0:16, :], in_=a.rearrange("s (j q) -> (s j) q", q=P))
        nc.sync.dma_start(out=rows[16:28, :], in_=c.rearrange("s (j q) -> (s j) q", q=P))
        vq = keep.tile([P, PASSES, C], U32, name="vq", align_bytes=64)
        nc.sync.dma_start(
            out=vq[:].bitcast(I32),
            in_=v_words.rearrange("g p n t -> p g (n t)").bitcast(I32),
        )
        vs = keep.tile([P, C], U8, name="vs", align_bytes=64)
        nc.vector.memset(vs[:].bitcast(I32), 0)
        for q in range(4):
            nc.sync.dma_start(
                out=vs[32 * q : 32 * q + 8, :].bitcast(I32),
                in_=v_scales[:, 4 * q : 4 * q + 4, :].bitcast(I32),
            )
        load_x(1, 0, 2)
        load_x(1, 2, 2)
        sk = {}
        for n in range(SEQS):
            sk[n] = keep.tile([P, 4, C], BF16, name=f"skip{n}")
            nc.sync.dma_start(out=sk[n][:], in_=skip[n].rearrange("(i p) c -> p i c", p=P))
            if n == 0:
                uq = keep.tile([P, F], U32, name="uq", align_bytes=64)
                nc.sync.dma_start(
                    out=uq[:].bitcast(I32), in_=u_words[0].rearrange("p n t -> p (n t)").bitcast(I32)
                )
                us = keep.tile([P, F], U8, name="us", align_bytes=64)
                nc.vector.memset(us[:].bitcast(I32), 0)
                for q in range(4):
                    nc.sync.dma_start(
                        out=us[32 * q : 32 * q + 4, :].bitcast(I32),
                        in_=u_scales[0, 4 * q : 4 * q + 4, :].bitcast(I32),
                    )
                bias = keep.tile([P, F], BF16, name="bias")
                nc.sync.dma_start(out=bias[:], in_=b.partition_broadcast(P))

        ident = keep.tile([P, P], F32, name="ident")
        make_identity(nc, ident[:])
        ident16 = keep.tile([P, P], BF16, name="ident16")
        nc.gpsimd.tensor_copy(out=ident16[:], in_=ident[:])
        one = keep.tile([P, 28], F32, name="one")
        nc.gpsimd.memset(one[:], 0.0)
        nc.gpsimd.memset(one[:, 0:BLOCKS], 1.0)

        y, ps = {}, {}
        for n in range(SEQS):
            for j in range(BLOCKS):
                planes = len(MERGED_TAPS[n]) + len(PLANE_TAPS[n])
                y[n, j] = keep.tile([P, planes, FRAMES], F32, name=f"y{n}{j}")
                for q, pair in enumerate(MERGED_TAPS[n]):
                    if pair[0][1] > 0:
                        nc.gpsimd.memset(y[n, j][:, q, 0 : pair[0][1]], 0.0)
                ps[n, j] = keep.tile([P, PAD + FRAMES + PAD], F32, name=f"ps{n}{j}")
                nc.gpsimd.memset(ps[n, j][:, 0:PAD], 0.0)
                nc.gpsimd.memset(ps[n, j][:, PAD + FRAMES :], 0.0)

        w = keep.tile([P, 28], F32, name="w")
        wbank = {}

        def w2():
            wbank[0] = psum.tile([P, 512], F32, name="mem", bufs=BANKS["mem"])
            nc.tensor.transpose(wbank[0][:].bitcast(BF16)[:, 0:P], rows[:], ident16[:])

        def w3():
            nc.vector.tensor_tensor(
                out=w[:], in0=wbank[0][:].bitcast(BF16)[:, 0:28], in1=one[:], op=ALU.add
            )

        x16, xbank, xg, xq, xqs = {}, {}, {}, {}, {}

        def turn_x(r):
            tag, bufs = (("acc", 3), ("acc", 3), ("acc", 3), ("mem", 2), ("turn", 1), ("acc", 3), ("acc", 3), ("acc", 3))[r]
            words = x16[r][:].bitcast(F32)
            xbank[r] = psum.tile([P, 512], F32, name=tag, bufs=bufs)
            for g in range(PASSES):
                for u in range(2):
                    nc.tensor.transpose(
                        xbank[r][:, 256 * g + 128 * u : 256 * g + 128 * u + 128],
                        words[:, 256 * g + u : 256 * g + 256 : 2],
                        ident[:],
                    )

        def copy(engine, out, in_):
            if engine == "vector":
                nc.vector.tensor_copy(out=out, in_=in_)
            else:
                nc.scalar.copy(out=out, in_=in_)

        def cast(r, engine):
            x16[r] = work.tile([P, D], BF16, name="x16", bufs=5)
            copy(engine, x16[r][:], xb8[r].bitcast(FP8))

        def scale_x(r):
            pair, k = divmod(r, 2)
            if pair not in xg:
                xg[pair] = work.tile([P, PASSES, HALF, 4], BF16, name="xg", bufs=3, align_bytes=64)
            for g in range(PASSES):
                nc.vector.tensor_tensor(
                    out=xg[pair][:, g, P * k : P * k + P, :].rearrange("p r (u e) -> p r u e", u=2),
                    in0=xbank[r][:, 256 * g : 256 * g + 256]
                    .bitcast(BF16)
                    .rearrange("p (u r e) -> p r u e", u=2, e=2),
                    in1=xs[:, g, :]
                    .rearrange("p (o u e) -> p o u e", o=1, u=2)
                    .to_broadcast([P, P, 2, 2]),
                    op=ALU.mult,
                )

        def quantize_x(pair):
            xq[pair] = keep.tile([P, PASSES, HALF], U32, name=f"xq{pair}", align_bytes=64)
            xqs[pair] = keep.tile([P, PASSES, HALF], U8, name=f"xqs{pair}", align_bytes=64)
            nc.vector.quantize_mx(
                out=xq[pair][:].rearrange("p g r -> p (g r)").bitcast(FP8X4),
                scales=xqs[pair][:].rearrange("p g r -> p (g r)"),
                in_=xg[pair][:].rearrange("p g r k -> p (g r k)"),
            )

        proj = {}

        def project(n, j):
            proj[n, j] = psum.tile([P, FRAMES], F32, name="proj", bufs=BANKS["proj"])
            for h in range(2):
                pair = 2 * n + h
                for g in range(PASSES):
                    nc.tensor.matmul_mx(
                        out=proj[n, j][:, HALF * h : HALF * h + HALF],
                        lhsT=vq[:, g, P * j : P * j + P].bitcast(FP8X4),
                        lhsT_scale=vs[4 * g : P, P * j : P * j + P],
                        rhs=xq[pair][:, g, :].bitcast(FP8X4),
                        rhs_scale=xqs[pair][:, g, :],
                        start=(g == 0),
                        stop=(g == PASSES - 1),
                    )

        def weight(tap, j):
            return w[:, 4 * tap[0] + j : 4 * tap[0] + j + 1]

        def keep_p(n, j, engine):
            copy(engine, ps[n, j][:, PAD : PAD + FRAMES], proj[n, j][:])

        def merged_taps(n, j, q):
            pair = MERGED_TAPS[n][q]
            for k, (row, d) in enumerate(pair):
                lo, hi = max(0, d), min(FRAMES, FRAMES + d)
                dst = y[n, j][:, q, lo:hi]
                src = proj[n, j][:, lo - d : hi - d]
                if k == 0:
                    nc.vector.tensor_scalar(
                        out=dst, in0=src, scalar1=weight((row, d), j), scalar2=None, op0=ALU.mult
                    )
                else:
                    nc.vector.scalar_tensor_tensor(
                        out=dst, in0=src, scalar=weight((row, d), j), in1=dst, op0=ALU.mult, op1=ALU.add
                    )

        def plane_tap(n, part, j, q, engine):
            tap, width = PLANE_TAPS[n][q], WIDTH[n]
            lo = width * part
            dst = y[n, j][:, len(MERGED_TAPS[n]) + q, lo : lo + width]
            src = ps[n, j][:, PAD + lo - tap[1] : PAD + lo - tap[1] + width]
            if engine == "scalar":
                nc.scalar.activation(out=dst, in_=src, func=ACT.Copy, scale=weight(tap, j))
            elif engine == "vector":
                nc.vector.tensor_scalar(out=dst, in0=src, scalar1=weight(tap, j), scalar2=None, op0=ALU.mult)
            else:
                nc.gpsimd.tensor_scalar(
                    out=dst, in0=src, scalar1=weight(tap, j), scalar2=0.0, op0=ALU.mult, op1=ALU.add
                )

        mem = {}

        def open_mem(i):
            n, k = divmod(i, 4)
            mem[i] = psum.tile([P, C], F32, name="mem", bufs=BANKS["mem"])
            nc.tensor.matmul(mem[i][:], ident16[:], sk[n][:, k, :], start=True, stop=False)

        def gather(i, j):
            n, k = divmod(i, 4)
            planes = y[n, j].shape[1]
            for q in range(planes):
                nc.tensor.matmul(
                    mem[i][:, P * j : P * j + P],
                    y[n, j][:, q, P * k : P * k + P],
                    ident[:],
                    start=False,
                    stop=(j == BLOCKS - 1 and q == planes - 1),
                    is_transpose=True,
                )

        m16, turned, mg, mq, ms = {}, {}, {}, {}, {}

        def round_m(i, engine):
            m16[i] = work.tile([P, C], BF16, name="m16", bufs=3)
            copy(
                engine,
                m16[i][:].rearrange("p (u w e) -> p u w e", u=2, e=2),
                mem[i][:].rearrange("p (w u e) -> p u w e", u=2, e=2),
            )

        def turn_m(i):
            words = m16[i][:].bitcast(F32)
            turned[i] = psum.tile([P, 512], F32, name="turn", bufs=BANKS["turn"])
            for u in range(2):
                nc.tensor.transpose(
                    turned[i][:, P * u : P * u + P], words[:, P * u : P * u + P], ident[:]
                )

        def lay_m(i, engine):
            mg[i] = work.tile([P, P, 4], BF16, name="mg", bufs=3, align_bytes=64)
            copy(
                engine,
                mg[i][:].rearrange("p r k -> p (r k)").bitcast(F32).rearrange("p (r u) -> p r u", u=2),
                turned[i][:, 0:256].rearrange("p (u r) -> p r u", u=2),
            )

        def quantize_m(i):
            mq[i] = work.tile([P, P], U32, name="mq", bufs=4, align_bytes=64)
            ms[i] = work.tile([P, P], U8, name="ms", bufs=4, align_bytes=64)
            nc.vector.quantize_mx(
                out=mq[i][:].bitcast(FP8X4), scales=ms[i][:], in_=mg[i][:].rearrange("p r k -> p (r k)")
            )

        acc, o = {}, {}

        def expand(i, f):
            tag = "proj" if 4 * i + f >= 4 and (4 * i + f) % 5 in SPARE else "acc"
            acc[i, f] = psum.tile([P, 512], F32, name=tag, bufs=BANKS[tag])
            nc.tensor.matmul_mx(
                out=acc[i, f][:],
                lhsT=mq[i][:].bitcast(FP8X4),
                lhsT_scale=ms[i][:],
                rhs=uq[:, 512 * f : 512 * f + 512].bitcast(FP8X4),
                rhs_scale=us[:, 512 * f : 512 * f + 512],
                start=True,
                stop=True,
            )

        def finish(i, lo, hi):
            if i not in o:
                o[i] = work.tile([P, F], F32, name="o", bufs=5)
            f, at = divmod(lo, 512)
            nc.vector.tensor_tensor(
                out=o[i][:, lo:hi], in0=acc[i, f][:, at : at + hi - lo], in1=bias[:, lo:hi], op=ALU.add
            )

        def relu(i, lo, hi, engine):
            piece = o[i][:, lo:hi]
            if engine == "scalar":
                nc.scalar.activation(out=piece, in_=piece, func=ACT.Relu)
            elif engine == "vector":
                nc.vector.tensor_scalar(out=piece, in0=piece, scalar1=0.0, scalar2=None, op0=ALU.max)
            else:
                nc.gpsimd.tensor_scalar(out=piece, in0=piece, scalar1=BIG, scalar2=0.0, op0=ALU.min, op1=ALU.max)

        def store(i, lo, hi):
            n, k = divmod(i, 4)
            wide = slice(lo, hi)
            nc.sync.dma_start(out=out[n, P * k : P * k + P, wide], in_=o[i][:, wide])

        with tc.manual_schedule():
            cast(0, "vector")
            turn_x(0)
            scale_x(0)
            cast(1, "scalar")
            turn_x(1)
            scale_x(1)
            cast(3, "scalar")
            cast(2, "scalar")
            turn_x(3)
            scale_x(3)
            turn_x(2)
            scale_x(2)
            quantize_x(0)
            w2()
            w3()
            cast(4, "scalar")
            turn_x(4)
            cast(5, "scalar")
            turn_x(5)
            open_mem(0)
            cast(6, "scalar")
            quantize_x(1)
            project(0, 1)
            scale_x(4)
            project(0, 3)
            scale_x(5)
            cast(7, "scalar")
            turn_x(7)
            keep_p(0, 1, "scalar")
            plane_tap(0, 1, 1, 1, "vector")
            plane_tap(0, 0, 1, 6, "vector")
            project(0, 0)
            scale_x(7)
            open_mem(1)
            plane_tap(0, 0, 1, 0, "gpsimd")
            keep_p(0, 3, "scalar")
            plane_tap(0, 0, 3, 0, "gpsimd")
            plane_tap(0, 0, 1, 2, "scalar")
            plane_tap(0, 0, 1, 4, "scalar")
            project(0, 2)
            quantize_x(2)
            plane_tap(0, 0, 1, 3, "scalar")
            turn_x(6)
            scale_x(6)
            keep_p(0, 0, "scalar")
            plane_tap(0, 0, 0, 0, "gpsimd")
            keep_p(0, 2, "scalar")
            plane_tap(0, 0, 2, 0, "gpsimd")
            plane_tap(0, 0, 3, 2, "scalar")
            plane_tap(0, 0, 1, 5, "vector")
            quantize_x(3)
            project(1, 3)
            plane_tap(0, 0, 2, 2, "scalar")
            plane_tap(0, 0, 0, 1, "scalar")
            plane_tap(0, 0, 2, 5, "vector")
            plane_tap(0, 0, 3, 1, "scalar")
            plane_tap(0, 0, 2, 6, "vector")
            project(1, 0)
            plane_tap(0, 1, 0, 3, "vector")
            plane_tap(0, 0, 0, 2, "scalar")
            plane_tap(0, 0, 0, 5, "vector")
            plane_tap(0, 0, 2, 1, "scalar")
            plane_tap(0, 0, 0, 6, "vector")
            plane_tap(0, 0, 0, 3, "scalar")
            plane_tap(0, 0, 1, 1, "scalar")
            plane_tap(0, 0, 0, 4, "scalar")
            plane_tap(0, 1, 0, 5, "vector")
            plane_tap(0, 1, 0, 0, "vector")
            gather(0, 0)
            plane_tap(0, 0, 2, 4, "scalar")
            plane_tap(0, 0, 3, 5, "vector")
            gather(0, 1)
            plane_tap(0, 1, 0, 2, "vector")
            plane_tap(0, 0, 3, 6, "vector")
            plane_tap(0, 1, 0, 1, "vector")
            plane_tap(0, 1, 0, 6, "vector")
            keep_p(1, 3, "scalar")
            plane_tap(1, 1, 3, 1, "gpsimd")
            merged_taps(1, 3, 0)
            plane_tap(0, 1, 1, 6, "vector")
            plane_tap(0, 1, 1, 0, "vector")
            plane_tap(0, 0, 2, 3, "scalar")
            plane_tap(0, 1, 2, 0, "vector")
            plane_tap(0, 1, 2, 3, "vector")
            plane_tap(0, 1, 1, 3, "vector")
            plane_tap(0, 0, 3, 3, "scalar")
            plane_tap(0, 0, 3, 4, "scalar")
            gather(0, 2)
            gather(0, 3)
            plane_tap(0, 1, 2, 5, "vector")
            plane_tap(0, 1, 1, 5, "vector")
            plane_tap(0, 1, 0, 4, "scalar")
            gather(1, 0)
            project(1, 2)
            keep_p(1, 0, "scalar")
            round_m(0, "scalar")
            open_mem(2)
            gather(2, 0)
            plane_tap(0, 1, 2, 4, "scalar")
            plane_tap(0, 1, 1, 2, "vector")
            plane_tap(0, 1, 1, 4, "scalar")
            plane_tap(0, 1, 3, 4, "scalar")
            plane_tap(1, 0, 0, 1, "scalar")
            plane_tap(0, 1, 2, 6, "vector")
            plane_tap(0, 1, 2, 2, "vector")
            plane_tap(0, 1, 3, 2, "vector")
            plane_tap(0, 1, 2, 1, "vector")
            turn_m(0)
            plane_tap(0, 1, 3, 5, "vector")
            keep_p(1, 2, "scalar")
            plane_tap(0, 1, 3, 3, "vector")
            lay_m(0, "scalar")
            plane_tap(0, 1, 3, 6, "vector")
            plane_tap(0, 1, 3, 0, "vector")
            gather(1, 1)
            gather(2, 1)
            gather(2, 2)
            quantize_m(0)
            plane_tap(1, 0, 0, 3, "scalar")
            gather(1, 2)
            plane_tap(1, 0, 2, 3, "scalar")
            plane_tap(0, 1, 3, 1, "vector")
            gather(1, 3)
            merged_taps(1, 0, 0)
            merged_taps(1, 2, 0)
            plane_tap(1, 0, 3, 1, "scalar")
            gather(2, 3)
            expand(0, 3)
            plane_tap(1, 0, 3, 2, "gpsimd")
            plane_tap(1, 0, 3, 4, "scalar")
            plane_tap(1, 0, 3, 0, "scalar")
            expand(0, 1)
            plane_tap(1, 0, 2, 0, "scalar")
            round_m(1, "scalar")
            plane_tap(1, 1, 0, 0, "gpsimd")
            plane_tap(1, 0, 0, 2, "gpsimd")
            plane_tap(1, 0, 0, 4, "scalar")
            plane_tap(1, 1, 2, 4, "scalar")
            project(1, 1)
            expand(0, 0)
            open_mem(3)
            turn_m(1)
            round_m(2, "scalar")
            plane_tap(1, 1, 3, 2, "gpsimd")
            keep_p(1, 1, "scalar")
            plane_tap(1, 1, 2, 1, "gpsimd")
            gather(3, 0)
            gather(3, 1)
            lay_m(1, "scalar")
            turn_m(2)
            plane_tap(1, 1, 0, 1, "gpsimd")
            finish(0, 512, 1024)
            plane_tap(1, 0, 1, 0, "scalar")
            plane_tap(1, 1, 3, 0, "gpsimd")
            finish(0, 1536, 2048)
            gather(3, 2)
            gather(3, 3)
            plane_tap(1, 0, 0, 0, "scalar")
            plane_tap(1, 0, 1, 3, "scalar")
            expand(0, 2)
            plane_tap(1, 1, 1, 1, "gpsimd")
            finish(0, 0, 512)
            lay_m(2, "scalar")
            merged_taps(1, 1, 0)
            plane_tap(1, 1, 1, 3, "gpsimd")
            relu(0, 0, 1024, "scalar")
            open_mem(4)
            plane_tap(1, 1, 2, 2, "gpsimd")
            quantize_m(2)
            expand(2, 0)
            quantize_m(1)
            expand(1, 3)
            expand(2, 1)
            plane_tap(1, 0, 2, 2, "gpsimd")
            round_m(3, "scalar")
            finish(0, 1024, 1536)
            expand(1, 2)
            expand(1, 1)
            plane_tap(1, 0, 1, 1, "scalar")
            turn_m(3)
            finish(2, 0, 512)
            plane_tap(1, 1, 0, 3, "gpsimd")
            plane_tap(1, 0, 1, 2, "gpsimd")
            plane_tap(1, 1, 2, 3, "gpsimd")
            plane_tap(1, 1, 0, 2, "gpsimd")
            gather(4, 0)
            finish(2, 512, 1024)
            plane_tap(1, 0, 1, 4, "scalar")
            gather(4, 1)
            plane_tap(1, 0, 2, 4, "scalar")
            plane_tap(1, 0, 2, 1, "scalar")
            gather(4, 2)
            plane_tap(1, 0, 3, 3, "scalar")
            gather(4, 3)
            store(0, 0, 1024)
            finish(1, 512, 1024)
            lay_m(3, "scalar")
            finish(1, 1536, 2048)
            plane_tap(1, 1, 1, 2, "gpsimd")
            quantize_m(3)
            expand(2, 3)
            expand(1, 0)
            relu(0, 1024, 2048, "scalar")
            plane_tap(1, 1, 1, 0, "gpsimd")
            expand(3, 2)
            store(0, 1024, 2048)
            finish(1, 1024, 1536)
            relu(1, 1024, 2048, "vector")
            store(1, 1024, 2048)
            finish(3, 1024, 1536)
            finish(1, 0, 512)
            open_mem(5)
            plane_tap(1, 1, 2, 0, "gpsimd")
            expand(3, 3)
            expand(3, 1)
            round_m(4, "scalar")
            plane_tap(1, 1, 0, 4, "scalar")
            turn_m(4)
            finish(3, 512, 1024)
            plane_tap(1, 1, 3, 4, "scalar")
            gather(5, 0)
            plane_tap(1, 1, 1, 4, "scalar")
            gather(5, 1)
            gather(5, 2)
            plane_tap(1, 1, 3, 3, "gpsimd")
            lay_m(4, "scalar")
            gather(5, 3)
            quantize_m(4)
            relu(2, 0, 1024, "scalar")
            finish(2, 1536, 2048)
            store(2, 0, 1024)
            expand(2, 2)
            expand(3, 0)
            finish(3, 1536, 2048)
            finish(2, 1024, 1536)
            expand(4, 2)
            finish(4, 1024, 1536)
            open_mem(6)
            expand(4, 0)
            finish(4, 0, 512)
            relu(1, 0, 1024, "scalar")
            store(1, 0, 1024)
            round_m(5, "scalar")
            expand(4, 3)
            expand(4, 1)
            finish(4, 512, 1024)
            finish(3, 0, 512)
            relu(2, 1024, 2048, "scalar")
            turn_m(5)
            lay_m(5, "scalar")
            relu(4, 0, 1024, "scalar")
            gather(6, 0)
            relu(3, 1024, 2048, "gpsimd")
            gather(6, 1)
            gather(6, 2)
            gather(6, 3)
            open_mem(7)
            quantize_m(5)
            expand(5, 3)
            expand(5, 2)
            store(3, 1024, 2048)
            finish(4, 1536, 2048)
            relu(3, 0, 1024, "gpsimd")
            expand(5, 1)
            expand(5, 0)
            round_m(6, "scalar")
            turn_m(6)
            lay_m(6, "scalar")
            finish(5, 1536, 2048)
            finish(5, 1024, 1536)
            finish(5, 0, 512)
            relu(4, 1024, 2048, "gpsimd")
            quantize_m(6)
            gather(7, 0)
            gather(7, 1)
            gather(7, 2)
            gather(7, 3)
            finish(5, 512, 1024)
            relu(5, 0, 1024, "gpsimd")
            store(2, 1024, 2048)
            store(4, 0, 1024)
            relu(5, 1536, 2048, "scalar")
            expand(6, 3)
            finish(6, 1536, 2048)
            relu(6, 1536, 2048, "gpsimd")
            store(3, 0, 1024)
            expand(6, 0)
            store(4, 1024, 2048)
            expand(6, 2)
            relu(5, 1024, 1536, "scalar")
            store(5, 1024, 2048)
            round_m(7, "scalar")
            turn_m(7)
            lay_m(7, "scalar")
            finish(6, 1024, 1536)
            relu(6, 1024, 1536, "scalar")
            finish(6, 0, 512)
            relu(6, 0, 512, "scalar")
            quantize_m(7)
            store(5, 0, 1024)
            store(6, 1024, 1536)
            store(6, 1536, 2048)
            expand(6, 1)
            finish(6, 512, 1024)
            relu(6, 512, 1024, "scalar")
            store(6, 0, 1024)
            expand(7, 3)
            finish(7, 1792, 2048)
            expand(7, 1)
            relu(7, 1792, 2048, "gpsimd")
            store(7, 1792, 2048)
            finish(7, 512, 1024)
            relu(7, 512, 1024, "scalar")
            expand(7, 2)
            expand(7, 0)
            finish(7, 1024, 1536)
            finish(7, 1536, 1792)
            relu(7, 1024, 1536, "vector")
            store(7, 512, 1024)
            store(7, 1024, 1536)
            finish(7, 0, 512)
            relu(7, 1536, 1792, "scalar")
            store(7, 1536, 1792)
            relu(7, 0, 512, "vector")
            store(7, 0, 512)
